import numpy as np
import ml_dtypes


def mxq(x, axis, fmt="e4m3"):
    dtype, down = {"e4m3": (ml_dtypes.float8_e4m3fn, 7), "e5m2": (ml_dtypes.float8_e5m2, 14)}[fmt]
    v = np.moveaxis(np.asarray(x, np.float32).astype(ml_dtypes.bfloat16).astype(np.float64), axis, -1)
    blocks = v.reshape(v.shape[:-1] + (-1, 32))
    amax = np.abs(blocks).max(-1, keepdims=True)
    byte = np.maximum(np.where(amax > 0, np.frexp(amax)[1] - 1 + 127, 0) - down, 1)
    scale = np.exp2(byte - 127.0)
    codes = (blocks / scale).astype(np.float32).astype(dtype).astype(np.float64)
    return np.moveaxis((codes * scale).reshape(v.shape), -1, axis)


WIDE = False


def mx_kscale(k):
    if not WIDE:
        return np.ones(k)
    levels = np.array([10, -10, 5, -5, 0])
    if k % 512:
        return np.exp2(np.random.permutation(np.resize(levels, k // 32))).repeat(32)
    a = np.empty((k // 512, 16))
    for p in range(k // 512):
        a[p, :8] = np.random.permutation(np.resize(levels, 8))
        for g in range(8):
            far = levels[np.abs(levels - a[p, g]) >= 10]
            a[p, g + 8] = far[np.random.randint(len(far))]
    return np.exp2(a.ravel()).repeat(32)


BF16 = ml_dtypes.bfloat16


def bf(x):
    return np.asarray(x, np.float32).astype(BF16)


def f64(x):
    return np.asarray(x).astype(np.float64)


E2M1 = np.array([0.0, 0.5, 1.0, 1.5, 2.0, 3.0, 4.0, 6.0, -0.0, -0.5, -1.0, -1.5, -2.0, -3.0, -4.0, -6.0])


def pack_weight(w, fmt):
    k, n = w.shape
    w = f64(bf(w)).reshape(k // 32, 32, n)
    amax = np.abs(w).max(1)
    if fmt == "e4m3":
        byte = np.frexp(amax)[1] - 1 + 127 - 7
    else:
        mant, ex = np.frexp(amax / 6.0)
        byte = np.where(mant > 0.5, ex, ex - 1) + 127
    byte = np.clip(np.where(amax > 0, byte, 1), 1, 254)
    scaled = (w * np.exp2(127.0 - byte)[:, None, :]).reshape(k, n).astype(np.float32)
    by_word = np.ascontiguousarray(scaled.reshape(k // 512, 128, 4, n).transpose(0, 1, 3, 2))
    if fmt == "e4m3":
        words = by_word.astype(ml_dtypes.float8_e4m3fn).view(np.uint8)
    else:
        c = by_word.astype(ml_dtypes.float4_e2m1fn).view(np.uint8) & 0xF
        words = c[..., 0::2] | (c[..., 1::2] << 4)
    return np.ascontiguousarray(words), np.ascontiguousarray(byte.astype(np.uint8).reshape(k // 512, 16, n))


def unpack_weight(words, scales, fmt):
    g, p, n, _ = words.shape
    if fmt == "e4m3":
        vals = np.ascontiguousarray(words).view(ml_dtypes.float8_e4m3fn).astype(np.float64)
    else:
        nib = np.empty((g, p, n, 4), np.uint8)
        nib[..., 0::2] = words & 0xF
        nib[..., 1::2] = words >> 4
        vals = E2M1[nib]
    vals = vals * np.repeat(np.exp2(scales.astype(np.float64) - 127.0), 8, axis=1)[..., None]
    return vals.transpose(0, 1, 3, 2).reshape(g * 512, n)
def pack4(w):
    words, scales = pack_weight(w, "e2m1")
    return words.reshape(words.shape[0], 128, -1), scales


def unpack4(words, scales):
    return unpack_weight(words.reshape(words.shape[0], 128, -1, 2), scales, "e2m1")


B, N, M = 1024, 1024, 512


def sigmoid(v):
    return 1.0 / (1.0 + np.exp(-v))


def draw0():
    p = mx_kscale(M)
    t = mx_kscale(N)
    x0 = bf(np.random.standard_normal((B, N)))
    inp = bf(np.random.standard_normal((B, M)) * p)
    u_words, u_scales = pack4(np.random.standard_normal((N, N)) * 2.0 / np.sqrt(N) / t[:, None])
    w_words, w_scales = pack4(np.random.standard_normal((M, N)) / np.sqrt(M) / p[:, None])
    return {
        "x0": x0,
        "inp": inp,
        "u_words": u_words,
        "u_scales": u_scales,
        "w_words": w_words,
        "w_scales": w_scales,
        "b": bf(np.random.standard_normal(N) * 0.5),
        "arev": bf(np.random.standard_normal(N) * 2.0),
        "g": bf((1.0 + 0.25 * np.random.standard_normal(N)) * t),
    }


def fused_unfold(x, s, uq, arev, g):
    f = sigmoid((mxq(x * g, 1, "e4m3") @ uq) + s)
    return (x + f * arev) / (2.0 + f)


def core(x0, inp, u_words, u_scales, w_words, w_scales, b, arev, g):
    x0, arev, g = f64(x0), f64(arev), f64(g)
    uq = unpack4(u_words, u_scales)
    s = (mxq(f64(inp), 1, "e4m3") @ unpack4(w_words, w_scales)) + f64(b)
    x1 = fused_unfold(x0, s, uq, arev, g)
    x2 = fused_unfold(x1, s, uq, arev, g)
    return x2


def e4m3fn_bytes(y):
    return np.clip(np.asarray(y, np.float64), -448.0, 448.0).astype(np.float32).astype(ml_dtypes.float8_e4m3fn).view(np.uint8)


def e4m3fn_values(b):
    return np.asarray(b, np.uint8).view(ml_dtypes.float8_e4m3fn).astype(np.float64)


def setup_inputs():
    d = draw0()
    x0 = np.asarray(d['inp']).astype(np.float64)
    s = (np.max(np.abs(x0), axis=(0,), keepdims=True) / 448.0).astype(np.float32)
    out = {}
    for k, v in d.items():
        if k == 'inp':
            out['inp_bytes'] = e4m3fn_bytes(x0 / s.astype(np.float64))
            out['inp_scale'] = s
        else:
            out[k] = v
    return out


def reference(x0, inp_bytes, inp_scale, u_words, u_scales, w_words, w_scales, b, arev, g):
    return core(x0, e4m3fn_values(inp_bytes) * inp_scale.astype(np.float64), u_words, u_scales, w_words, w_scales, b, arev, g)

@@ -1,0 +1,430 @@
+from contextlib import ExitStack
+
+import concourse.mybir as mybir
+from concourse.masks import make_identity
+
+B, N, M = 1024, 1024, 512
+FLOPS = 2 * B * N * (M + 2 * N)
+
+F32 = mybir.dt.float32
+BF16 = mybir.dt.bfloat16
+I32 = mybir.dt.int32
+U32 = mybir.dt.uint32
+U8 = mybir.dt.uint8
+FP8 = mybir.dt.float8_e4m3fn
+FP8X4 = mybir.dt.float8_e4m3fn_x4
+FP4X4 = mybir.dt.float4_e2m1fn_x4
+ALU = mybir.AluOpType
+ACT = mybir.ActivationFunctionType
+
+P = 128
+PACK = 4
+K_PASS = P * PACK
+GROUPS = N // K_PASS
+SLICES = GROUPS * PACK
+SETS = 1 + GROUPS
+PAIR = 2 * P
+LN_3_2 = 0.4054651081081644
+
+BLOCK_TILES = (4, 4)
+LAG1 = 2
+LAG2 = 1
+CAST_ON_VECTOR = ((0, 0), (0, 1), (0, 2))
+EARLY = (4, 4)
+WARM = False
+EMIT_ON_VECTOR = ()
+ENG = mybir.EngineType
+MANUAL = {ENG.PE, ENG.SP, ENG.DVE, ENG.Activation}
+COPY_ON_VECTOR = ((1,1,1),(1,1,3))
+GAP_ON_SCALAR = ()
+BANKS = None
+LAGG = 10
+
+
+def tile_liquidtimeconstantfusedtwounfolds_w4_kernel(
+    tc, x0, inp_bytes, inp_scale, u_words, u_scales, w_words, w_scales, b, arev, g, out
+):
+    nc = tc.nc
+    blocks = len(BLOCK_TILES)
+    first_row = [P * sum(BLOCK_TILES[:i]) for i in range(blocks)]
+
+    def rows_of(hbm, blk):
+        tiles = BLOCK_TILES[blk]
+        return hbm[first_row[blk] : first_row[blk] + P * tiles, :].rearrange("(p j) k -> p j k", j=tiles)
+
+    with ExitStack() as ctx:
+        keep = ctx.enter_context(tc.tile_pool(name="keep", bufs=1))
+        work = ctx.enter_context(tc.tile_pool(name="work", bufs=3))
+        psum = ctx.enter_context(tc.psum_pool(name="psum", bufs=8))
+
+        if MANUAL:
+            ctx.enter_context(tc.manual_schedule(engines=MANUAL))
+
+        def bank(shape, role):
+            if BANKS is None:
+                return psum.tile(shape, F32, name="bank", tag="bank")
+            return psum.tile(shape, F32, name=role, tag=role, bufs=BANKS[role])
+
+        def per_channel(vec, name):
+            tile = keep.tile([P, GROUPS, PACK], BF16, name=name)
+            nc.scalar.dma_start(out=tile[:], in_=vec.rearrange("(g p t) -> p g t", p=P, t=PACK))
+            return tile[:].rearrange("p g t -> p (g t)")
+
+        scales_raw = keep.tile([P, SETS, N], U8, name="scales_raw")
+        nc.vector.memset(scales_raw[:].bitcast(I32), 0)
+
+        g_col = per_channel(g, "g_col")
+        identity = keep.tile([P, P], F32, name="identity")
+        make_identity(nc, identity[:])
+        inp_scale_col = keep.tile([P, PACK], F32, name="inp_scale_col")
+        nc.scalar.dma_start(out=inp_scale_col[:], in_=inp_scale.rearrange("o (p t) -> p (o t)", t=PACK))
+        a_col = per_channel(arev, "a_col")
+        b_col = per_channel(b, "b_col")
+
+        x0_rows = {}
+        inp_codes = {}
+        words_raw = {}
+
+        def load_x0(blk, pair):
+            tile = keep.tile([P, 2, N], BF16, name="x0_rows_%d_%d" % (blk, pair))
+            nc.sync.dma_start(out=tile[:], in_=rows_of(x0, blk)[:, 2 * pair : 2 * pair + 2, :])
+            x0_rows[blk, pair] = tile
+
+        def load_inp(blk):
+            tile = keep.tile([P, BLOCK_TILES[blk], M], U8, name="inp_codes_%d" % blk)
+            nc.sync.dma_start(out=tile[:], in_=rows_of(inp_bytes, blk))
+            inp_codes[blk] = tile
+
+        def load_words(grp):
+            tile = keep.tile([P, SETS, 2 * K_PASS], U8, name="words_raw_%d" % grp)
+            cols = slice(2 * K_PASS * grp, 2 * K_PASS * (grp + 1))
+            nc.sync.dma_start(out=tile[:, 0:1, :].bitcast(I32), in_=w_words.rearrange("g p n -> p g n")[:, :, cols].bitcast(I32))
+            nc.sync.dma_start(out=tile[:, 1:SETS, :].bitcast(I32), in_=u_words.rearrange("g p n -> p g n")[:, :, cols].bitcast(I32))
+            words_raw[grp] = tile
+
+        def load_scales():
+            for quad in range(4):
+                rows = slice(32 * quad, 32 * quad + 4)
+                src = slice(4 * quad, 4 * quad + 4)
+                nc.sync.dma_start(out=scales_raw[rows, 0:1, :].bitcast(I32), in_=w_scales.rearrange("g q n -> q g n")[src].bitcast(I32))
+                nc.sync.dma_start(out=scales_raw[rows, 1:SETS, :].bitcast(I32), in_=u_scales.rearrange("g q n -> q g n")[src].bitcast(I32))
+
+        def load_block(blk):
+            load_x0(blk, 0)
+            load_inp(blk)
+            for pair in range(1, BLOCK_TILES[blk] // 2):
+                load_x0(blk, pair)
+
+        load_words(0)
+        load_block(0)
+        load_scales()
+        load_block(1)
+        load_words(1)
+        for blk in range(2, blocks):
+            load_block(blk)
+
+        a_rows = None
+
+        if WARM:
+            warm = keep.tile([P, 1], F32, name="warm")
+            nc.scalar.activation(out=warm[:], in_=identity[:, 0:1], func=ACT.Sigmoid)
+
+        def scaled(col, factor, name):
+            tile = keep.tile([P, SLICES], F32, name=name)
+            nc.scalar.activation(out=tile[:], in_=col, func=ACT.Copy, scale=factor)
+            return tile
+
+        const = {}
+
+        def constants_scalar():
+            spread = bank([P, PACK, P], "turn")
+            for t in range(PACK):
+                nc.tensor.transpose(spread[:, t, :], inp_scale_col[:, t : t + 1].to_broadcast([P, P]), identity[:])
+            const["inp_scale"] = keep.tile([P, M], F32, name="inp_scale_rows")
+            nc.scalar.copy(out=const["inp_scale"][:].rearrange("p (m t) -> p m t", t=PACK), in_=spread[:].rearrange("p t m -> p m t"))
+            const["two_a"] = scaled(a_col, 2.0, "two_a")
+            const["a"] = scaled(a_col, 1.0, "a_f32")
+            const["a_sixth"] = scaled(a_col, 1.0 / 6.0, "a_sixth")
+            const["g_sixth"] = scaled(g_col, 1.0 / 6.0, "g_sixth")
+
+        def constants_vector():
+            const["a_g"] = keep.tile([P, SLICES], F32, name="a_g")
+            nc.vector.tensor_tensor(out=const["a_g"][:], in0=a_col, in1=g_col, op=ALU.mult)
+            const["bias"] = keep.tile([P, SLICES], F32, name="bias")
+            nc.vector.tensor_scalar(out=const["bias"][:], in0=b_col, scalar1=LN_3_2, scalar2=None, op0=ALU.add)
+
+        words = [keep.tile([P, SETS, 2 * P], U8, name="words_%d" % s, align_bytes=64) for s in range(SLICES)]
+        scales = [keep.tile([P, SETS, P], U8, name="scales_%d" % s, align_bytes=64) for s in range(SLICES)]
+
+        def regroup_words(s):
+            grp, t = divmod(s, PACK)
+            src = words_raw[grp][:].rearrange("p s (m t b) -> p s m t b", t=PACK, b=2)[:, :, :, t, :]
+            nc.vector.tensor_copy(out=words[s][:].rearrange("p s (m b) -> p s m b", b=2), in_=src)
+
+        def regroup_scales(s):
+            grp, t = divmod(s, PACK)
+            src = scales_raw[:].rearrange("p s (g m t) -> p s g m t", g=GROUPS, t=PACK)[:, :, grp, :, t]
+            nc.vector.tensor_copy(out=scales[s][:], in_=src)
+
+        quantised = {}
+
+        def quantise(key, grouped):
+            tokens = grouped.shape[1]
+            codes = keep.tile([P, tokens], U32, name="codes_%s_%d_%d" % key, align_bytes=64)
+            plane = keep.tile([P, tokens], U8, name="plane_%s_%d_%d" % key, align_bytes=64)
+            nc.vector.quantize_mx(out=codes[:].bitcast(FP8X4), scales=plane[:], in_=grouped[:].rearrange("p c t -> p (c t)"))
+            quantised[key] = (codes, plane)
+
+        def turn(rows, grp):
+            turned = bank([P, 2, PAIR], "turn")
+            for j in range(2):
+                row_words = rows[:, j, :].bitcast(F32)
+                for u in range(2):
+                    nc.tensor.transpose(
+                        turned[:, u, P * j : P * (j + 1)],
+                        row_words[:, 256 * grp + u : 256 * (grp + 1) : 2],
+                        identity[:],
+                    )
+            return turned[:]
+
+        def times_factor(dst, pair, turned, factor):
+            nc.vector.tensor_tensor(
+                out=dst[:, PAIR * pair : PAIR * (pair + 1), :].rearrange("p c (u e) -> p c u e", e=2),
+                in0=turned,
+                in1=factor.rearrange("p (u e) -> p u e", e=2).unsqueeze(1).to_broadcast([P, PAIR, 2, 2]),
+                op=ALU.mult,
+            )
+
+        gap = {}
+        rise = {}
+
+        grouped = {}
+        wide = {}
+        turned_x0 = {}
+        for blk in range(blocks):
+            tokens = P * BLOCK_TILES[blk]
+            for s in range(SLICES):
+                gap[blk, s] = keep.tile([P, tokens], F32, name="gap_%d_%d" % (blk, s))
+                rise[blk, s] = keep.tile([P, tokens], F32, name="rise_%d_%d" % (blk, s))
+            for i in range(SETS):
+                grouped[blk, i] = keep.tile([P, tokens, PACK], BF16, name="grouped_%d_%d" % (blk, i), align_bytes=64)
+
+        def widen(blk, pair):
+            wide[blk, pair] = keep.tile([P, 2, M], BF16, name="wide_%d_%d" % (blk, pair))
+            for j in range(2):
+                nc.vector.tensor_tensor(
+                    out=wide[blk, pair][:, j, :], in0=inp_codes[blk][:, 2 * pair + j, :].bitcast(FP8), in1=const["inp_scale"][:], op=ALU.mult
+                )
+
+        def turn_inp(blk, pair):
+            dst = grouped[blk, 0][:, PAIR * pair : PAIR * (pair + 1), :].rearrange("p c t -> p (c t)").bitcast(F32)
+            nc.scalar.copy(out=dst.rearrange("p (c u) -> p c u", u=2), in_=turn(wide[blk, pair], 0).rearrange("p u c -> p c u"))
+
+        def turn_x0(blk, grp, pair):
+            turned_x0[blk, grp, pair] = turn(x0_rows[blk, pair], grp).bitcast(BF16).rearrange("p u (c e) -> p c u e", e=2)
+
+        def times_g(blk, grp, pair):
+            times_factor(grouped[blk, 1 + grp], pair, turned_x0[blk, grp, pair], g_col[:, PACK * grp : PACK * (grp + 1)])
+
+        def first_gap(blk, grp, pair):
+            for t in range(PACK):
+                s = PACK * grp + t
+                nc.scalar.activation(
+                    out=gap[blk, s][:, PAIR * pair : PAIR * (pair + 1)],
+                    in_=turned_x0[blk, grp, pair][:, :, t // 2, t % 2],
+                    func=ACT.Identity,
+                    scale=-1.0,
+                    bias=const["two_a"][:, s : s + 1],
+                )
+
+        def quantise_input(blk, i):
+            quantise(("inp", blk, 0) if i == 0 else ("x0", blk, i - 1), grouped[blk, i])
+
+        gate = {}
+        sums = {}
+
+        def passes(unfold, blk, s, first, last):
+            if unfold == 1:
+                order = [(1, ("x0", blk, 0)), (2, ("x0", blk, 1)), (0, ("inp", blk, 0))]
+            else:
+                order = [(0, ("inp", blk, 0)), (1, ("x1", blk, 0)), (2, ("x1", blk, 1))]
+            if first == 0:
+                sums[unfold, blk, s] = bank([P, K_PASS], "sum")
+            for i in range(first, last):
+                weight, key = order[i]
+                codes, plane = quantised[key]
+                nc.tensor.matmul_mx(
+                    out=sums[unfold, blk, s][:],
+                    lhsT=words[s][:, weight, :].bitcast(FP4X4),
+                    lhsT_scale=scales[s][:, weight, :],
+                    rhs=codes[:].bitcast(FP8X4),
+                    rhs_scale=plane[:],
+                    start=(i == 0),
+                    stop=(i == SETS - 1),
+                )
+
+        def multiply(unfold, blk, s):
+            early = unfold == 2 and s < EARLY[blk]
+            passes(unfold, blk, s, SETS - 1 if early else 0, SETS)
+
+        def open_early(blk):
+            for i in range(SETS - 1):
+                for s in range(EARLY[blk]):
+                    passes(2, blk, s, i, i + 1)
+
+        def squash(unfold, blk, s):
+            tokens = P * BLOCK_TILES[blk]
+            acc = sums[unfold, blk, s]
+            h = work.tile([P, tokens], F32, name="gate", tag="gate", bufs=14)
+            nc.scalar.activation(out=h[:], in_=acc[:], func=ACT.Sigmoid, bias=const["bias"][:, s : s + 1])
+            gate[unfold, blk, s] = h
+
+        def step_state(unfold, blk, s):
+            nc.vector.scalar_tensor_tensor(
+                out=rise[blk, s][:], in0=gate[unfold, blk, s][:], scalar=-3.0, in1=gap[blk, s][:], op0=ALU.add, op1=ALU.mult
+            )
+
+        planes = {}
+        regrouped = {}
+
+        def cast(blk, s):
+            grp, t = divmod(s, PACK)
+            if t == 0:
+                planes[blk, grp] = work.tile([P, PACK, P * BLOCK_TILES[blk]], BF16, name="planes", tag="planes")
+            dst = planes[blk, grp][:, t, :]
+            factor, shift = const["g_sixth"][:, s : s + 1], const["a_g"][:, s : s + 1]
+            if (blk, s) in CAST_ON_VECTOR:
+                nc.vector.tensor_scalar(out=dst, in0=rise[blk, s][:], scalar1=factor, scalar2=shift, op0=ALU.mult, op1=ALU.add)
+            else:
+                nc.scalar.activation(out=dst, in_=rise[blk, s][:], func=ACT.Identity, scale=factor, bias=shift)
+
+        def interleave(blk, grp):
+            tile = work.tile([P, P * BLOCK_TILES[blk], PACK], BF16, name="x1_grouped", tag="x1_grouped", align_bytes=64)
+            nc.vector.tensor_copy(
+                out=tile[:].rearrange("p (c i) t -> p c t i", i=4), in_=planes[blk, grp][:].rearrange("p t (c i) -> p c t i", i=4)
+            )
+            regrouped[blk, grp] = tile
+
+        def next_gap(blk, s):
+            if blk in GAP_ON_SCALAR:
+                nc.scalar.activation(out=gap[blk, s][:], in_=rise[blk, s][:], func=ACT.Identity, scale=-1.0 / 36.0, bias=const["a_sixth"][:, s : s + 1])
+                return
+            nc.vector.tensor_scalar(
+                out=gap[blk, s][:], in0=rise[blk, s][:], scalar1=-1.0 / 36.0, scalar2=const["a_sixth"][:, s : s + 1], op0=ALU.mult, op1=ALU.add
+            )
+
+        turned_out = {}
+
+        def turn_out(blk, s, j):
+            grp, t = divmod(s, PACK)
+            if t == 0:
+                turned_out[blk, grp, j] = bank([P, PACK, P], "turn")
+            dst = turned_out[blk, grp, j][:, t, :]
+            alone = (blk, grp, j) in EMIT_ON_VECTOR
+            if not alone:
+                nc.tensor.matmul(out=dst, lhsT=const["a"][:, s : s + 1].to_broadcast([P, P]), rhs=identity[:], start=True, stop=False, is_transpose=True)
+            nc.tensor.matmul(out=dst, lhsT=rise[blk, s][:, P * j : P * (j + 1)], rhs=identity[:], start=alone, stop=True, is_transpose=True)
+
+        def store(blk, grp, j):
+            turned = turned_out[blk, grp, j]
+            result = work.tile([P, P, PACK], F32, name="result", tag="result", bufs=6)
+            if (blk, grp, j) in EMIT_ON_VECTOR:
+                a_part = a_rows[:, K_PASS * grp : K_PASS * (grp + 1)].rearrange("p (m t) -> p m t", t=PACK)
+                nc.vector.tensor_tensor(out=result[:], in0=turned[:].rearrange("p t m -> p m t"), in1=a_part, op=ALU.add)
+            elif (blk, grp, j) in COPY_ON_VECTOR:
+                nc.vector.tensor_copy(out=result[:], in_=turned[:].rearrange("p t m -> p m t"))
+            else:
+                nc.scalar.copy(out=result[:], in_=turned[:].rearrange("p t m -> p m t"))
+            nc.sync.dma_start(
+                out=rows_of(out, blk)[:, j, K_PASS * grp : K_PASS * (grp + 1)], in_=result[:].rearrange("p m t -> p (m t)")
+            )
+
+        def emit(blk, grp, j):
+            for t in range(PACK):
+                turn_out(blk, PACK * grp + t, j)
+            store(blk, grp, j)
+
+        def requantise(blk, grp):
+            quantise(("x1", blk, grp), regrouped[blk, grp])
+
+        parts = [(grp, pair) for pair in range(2) for grp in range(GROUPS)]
+
+        constants_scalar()
+        for s in range(PACK):
+            regroup_words(s)
+        for grp in range(GROUPS):
+            turn_x0(0, grp, 0)
+            times_g(0, grp, 0)
+            first_gap(0, grp, 0)
+        for grp in range(GROUPS):
+            turn_x0(0, grp, 1)
+        for pair in range(2):
+            widen(0, pair)
+            turn_inp(0, pair)
+        for grp in range(GROUPS):
+            times_g(0, grp, 1)
+            first_gap(0, grp, 1)
+        constants_vector()
+        quantise_input(0, 1)
+        regroup_scales(0)
+        quantise_input(0, 2)
+        quantise_input(0, 0)
+        regroup_scales(1)
+        for grp in range(GROUPS):
+            turn_x0(1, grp, 0)
+            times_g(1, grp, 0)
+
+        def regroup(s):
+            if s >= PACK:
+                regroup_words(s)
+            regroup_scales(s)
+
+        beside = {
+            0: [(regroup, 2), (regroup, 3)],
+            1: [(widen, 1, 0), (first_gap, 1, 0, 0), (turn_x0, 1, 0, 1), (regroup, 4)],
+            2: [(turn_inp, 1, 0), (turn_x0, 1, 1, 1), (widen, 1, 1), (regroup, 5)],
+            3: [(first_gap, 1, 1, 0), (turn_inp, 1, 1), (times_g, 1, 0, 1), (times_g, 1, 1, 1), (regroup, 6)],
+            4: [(quantise_input, 1, 1), (regroup, 7)],
+            5: [(first_gap, 1, 0, 1), (quantise_input, 1, 2), (quantise_input, 1, 0)],
+            7: [(first_gap, 1, 1, 1)],
+        }
+        for s in range(SLICES):
+            multiply(1, 0, s)
+            squash(1, 0, s)
+            for call in beside.get(s, []):
+                call[0](*call[1:])
+
+        for s in range(SLICES):
+            multiply(1, 1, s)
+        P1 = lambda b, s: (step_state, 1, b, s)
+        P2 = lambda b, s: (step_state, 2, b, s)
+        C = lambda b, s: (cast, b, s)
+        S1 = lambda b, s: (squash, 1, b, s)
+        S2 = lambda b, s: (squash, 2, b, s)
+        M2 = lambda b, s: (multiply, 2, b, s)
+        G = lambda b, s: (next_gap, b, s)
+        I = lambda b, s: (interleave, b, s)
+        Q = lambda b, s: (requantise, b, s)
+        E = lambda b, g, j: (emit, b, g, j)
+        seq = [
+            P1(0,0), P1(0,1), C(0,0), P1(0,2), C(0,1), P1(0,3), C(0,2), S1(1,0), C(0,3), P1(0,4), C(0,4), P1(0,5), C(0,5), I(0,0), S1(1,1), S1(1,2),
+            P1(0,6), C(0,6), Q(0,0), S1(1,3), (open_early, 0), P1(0,7), C(0,7), P1(1,0), C(1,0), P1(1,1), C(1,1), I(0,1), S1(1,4), S1(1,5), P1(1,2), Q(0,1), C(1,2),
+            M2(0,0), M2(0,1), M2(0,2), M2(0,3), M2(0,4), M2(0,5), S1(1,6), M2(0,6),
+            P1(1,3), C(1,3), P1(1,4), C(1,4), P1(1,5), C(1,5), I(1,0), S1(1,7), M2(0,7), S2(0,0), P1(1,6), C(1,6), Q(1,0), S2(0,1), P1(1,7), C(1,7),
+            S2(0,2), S2(0,3), (open_early, 1), G(0,0), G(0,1), G(0,2), I(1,1), P2(0,0), Q(1,1), S2(0,4), S2(0,5), S2(0,6), S2(0,7),
+            M2(1,0), M2(1,1), M2(1,2), M2(1,3), M2(1,4), M2(1,5),
+            G(0,3), P2(0,1), G(0,4), P2(0,2), P2(0,3), S2(1,0), S2(1,1), S2(1,2), S2(1,3), S2(1,4),
+            E(0,0,0), M2(1,6), S2(1,5), E(0,0,1), M2(1,7), S2(1,6), E(0,0,2), S2(1,7), E(0,0,3),
+            G(0,5), P2(0,4), G(0,6), P2(0,5), G(0,7), P2(0,6), G(1,0), P2(0,7),
+            E(0,1,0), E(0,1,1), E(0,1,2), E(0,1,3),
+            G(1,1), P2(1,0), G(1,2), P2(1,1), G(1,3), P2(1,2), G(1,4), P2(1,3),
+            E(1,0,0), E(1,0,1), E(1,0,2), E(1,0,3),
+            G(1,5), P2(1,4), G(1,6), P2(1,5), G(1,7), P2(1,6), P2(1,7),
+        ]
+        for call in seq:
+            call[0](*call[1:])
+        for s in range(PACK, SLICES):
+            for j in range(4):
+                turn_out(1, s, j)
+        for j in range(4):
+            store(1, 1, j)

@@ -29,13 +29,15 @@ LN_3_2 = 0.4054651081081644
 BLOCK_TILES = (4, 4)
 LAG1 = 2
 LAG2 = 1
-CAST_ON_VECTOR = ((0, 0), (0, 1), (0, 2))
-EARLY = (4, 4)
-WARM = False
-EMIT_ON_VECTOR = ()
+CAST_ON_VECTOR = ((0, 0), (0, 1), (0, 3), (0, 7), (1, 3), (1, 7))
+EARLY = {(1, 0): 3, (1, 1): 0, (2, 0): 4, (2, 1): 4}
+SOFF = 1
+EOFF = 4
+WARM = True
+EMIT_ON_VECTOR = ((1, 1, 1), (1, 1, 3))
 ENG = mybir.EngineType
 MANUAL = {ENG.PE, ENG.SP, ENG.DVE, ENG.Activation}
-COPY_ON_VECTOR = ((1,1,1),(1,1,3))
+COPY_ON_VECTOR = ((1, 1, 1), (1, 1, 3))
 GAP_ON_SCALAR = ()
 BANKS = None
 LAGG = 10
@@ -76,6 +78,8 @@ def tile_liquidtimeconstantfusedtwounfolds_w4_kernel(
         g_col = per_channel(g, "g_col")
         identity = keep.tile([P, P], F32, name="identity")
         make_identity(nc, identity[:])
+        identity_bf16 = keep.tile([P, P], BF16, name="identity_bf16")
+        make_identity(nc, identity_bf16[:])
         inp_scale_col = keep.tile([P, PACK], F32, name="inp_scale_col")
         nc.scalar.dma_start(out=inp_scale_col[:], in_=inp_scale.rearrange("o (p t) -> p (o t)", t=PACK))
         a_col = per_channel(arev, "a_col")
@@ -123,7 +127,6 @@ def tile_liquidtimeconstantfusedtwounfolds_w4_kernel(
         for blk in range(2, blocks):
             load_block(blk)
 
-        a_rows = None
 
         if WARM:
             warm = keep.tile([P, 1], F32, name="warm")
@@ -143,7 +146,11 @@ def tile_liquidtimeconstantfusedtwounfolds_w4_kernel(
             const["inp_scale"] = keep.tile([P, M], F32, name="inp_scale_rows")
             nc.scalar.copy(out=const["inp_scale"][:].rearrange("p (m t) -> p m t", t=PACK), in_=spread[:].rearrange("p t m -> p m t"))
             const["two_a"] = scaled(a_col, 2.0, "two_a")
-            const["a"] = scaled(a_col, 1.0, "a_f32")
+            spread_a = psum.tile([P, SLICES, P], BF16, name="bank", tag="bank")
+            for s in range(SLICES):
+                nc.tensor.transpose(spread_a[:, s, :], a_col[:, s : s + 1].to_broadcast([P, P]), identity_bf16[:])
+            const["a_rows"] = keep.tile([P, GROUPS, K_PASS], BF16, name="a_rows")
+            nc.scalar.copy(out=const["a_rows"][:].rearrange("p g n -> p (g n)"), in_=spread_a[:].rearrange("p s m -> p (s m)"))
             const["a_sixth"] = scaled(a_col, 1.0 / 6.0, "a_sixth")
             const["g_sixth"] = scaled(g_col, 1.0 / 6.0, "g_sixth")
 
@@ -153,18 +160,16 @@ def tile_liquidtimeconstantfusedtwounfolds_w4_kernel(
             const["bias"] = keep.tile([P, SLICES], F32, name="bias")
             nc.vector.tensor_scalar(out=const["bias"][:], in0=b_col, scalar1=LN_3_2, scalar2=None, op0=ALU.add)
 
-        words = [keep.tile([P, SETS, 2 * P], U8, name="words_%d" % s, align_bytes=64) for s in range(SLICES)]
-        scales = [keep.tile([P, SETS, P], U8, name="scales_%d" % s, align_bytes=64) for s in range(SLICES)]
+        words = [keep.tile([P, PACK, SETS, 2 * P], U8, name="words_%d" % grp, align_bytes=64) for grp in range(GROUPS)]
+        scales = [keep.tile([P, PACK, SETS, P], U8, name="scales_%d" % grp, align_bytes=64) for grp in range(GROUPS)]
 
-        def regroup_words(s):
-            grp, t = divmod(s, PACK)
-            src = words_raw[grp][:].rearrange("p s (m t b) -> p s m t b", t=PACK, b=2)[:, :, :, t, :]
-            nc.vector.tensor_copy(out=words[s][:].rearrange("p s (m b) -> p s m b", b=2), in_=src)
+        def regroup_words(grp):
+            src = words_raw[grp][:].rearrange("p s (m t b) -> p t s m b", t=PACK, b=2)
+            nc.vector.tensor_copy(out=words[grp][:].rearrange("p t s (m b) -> p t s m b", b=2), in_=src)
 
-        def regroup_scales(s):
-            grp, t = divmod(s, PACK)
-            src = scales_raw[:].rearrange("p s (g m t) -> p s g m t", g=GROUPS, t=PACK)[:, :, grp, :, t]
-            nc.vector.tensor_copy(out=scales[s][:], in_=src)
+        def regroup_scales(grp):
+            src = scales_raw[:].rearrange("p s (g m t) -> p g t s m", g=GROUPS, t=PACK)[:, grp]
+            nc.vector.tensor_copy(out=scales[grp][:], in_=src)
 
         quantised = {}
 
@@ -199,13 +204,18 @@ def tile_liquidtimeconstantfusedtwounfolds_w4_kernel(
         rise = {}
 
         grouped = {}
+        gap2 = {}
+        rise2 = {}
         wide = {}
         turned_x0 = {}
         for blk in range(blocks):
             tokens = P * BLOCK_TILES[blk]
-            for s in range(SLICES):
-                gap[blk, s] = keep.tile([P, tokens], F32, name="gap_%d_%d" % (blk, s))
-                rise[blk, s] = keep.tile([P, tokens], F32, name="rise_%d_%d" % (blk, s))
+            for r in range(SLICES // 2):
+                gap2[blk, r] = keep.tile([P, 2, tokens], F32, name="gap_%d_%d" % (blk, r))
+                rise2[blk, r] = keep.tile([P, 2, tokens], F32, name="rise_%d_%d" % (blk, r))
+                for i in range(2):
+                    gap[blk, 2 * r + i] = gap2[blk, r][:, i, :]
+                    rise[blk, 2 * r + i] = rise2[blk, r][:, i, :]
             for i in range(SETS):
                 grouped[blk, i] = keep.tile([P, tokens, PACK], BF16, name="grouped_%d_%d" % (blk, i), align_bytes=64)
 
@@ -244,8 +254,10 @@ def tile_liquidtimeconstantfusedtwounfolds_w4_kernel(
         sums = {}
 
         def passes(unfold, blk, s, first, last):
-            if unfold == 1:
+            if (unfold, blk) == (1, 1):
                 order = [(1, ("x0", blk, 0)), (2, ("x0", blk, 1)), (0, ("inp", blk, 0))]
+            elif unfold == 1:
+                order = [(0, ("inp", blk, 0)), (1, ("x0", blk, 0)), (2, ("x0", blk, 1))]
             else:
                 order = [(0, ("inp", blk, 0)), (1, ("x1", blk, 0)), (2, ("x1", blk, 1))]
             if first == 0:
@@ -255,8 +267,8 @@ def tile_liquidtimeconstantfusedtwounfolds_w4_kernel(
                 codes, plane = quantised[key]
                 nc.tensor.matmul_mx(
                     out=sums[unfold, blk, s][:],
-                    lhsT=words[s][:, weight, :].bitcast(FP4X4),
-                    lhsT_scale=scales[s][:, weight, :],
+                    lhsT=words[s // PACK][:, s % PACK, weight, :].bitcast(FP4X4),
+                    lhsT_scale=scales[s // PACK][:, s % PACK, weight, :],
                     rhs=codes[:].bitcast(FP8X4),
                     rhs_scale=plane[:],
                     start=(i == 0),
@@ -264,24 +276,24 @@ def tile_liquidtimeconstantfusedtwounfolds_w4_kernel(
                 )
 
         def multiply(unfold, blk, s):
-            early = unfold == 2 and s < EARLY[blk]
+            early = s < EARLY[unfold, blk]
             passes(unfold, blk, s, SETS - 1 if early else 0, SETS)
 
-        def open_early(blk):
+        def open_early(unfold, blk):
             for i in range(SETS - 1):
-                for s in range(EARLY[blk]):
-                    passes(2, blk, s, i, i + 1)
+                for s in range(EARLY[unfold, blk]):
+                    passes(unfold, blk, s, i, i + 1)
 
         def squash(unfold, blk, s):
-            tokens = P * BLOCK_TILES[blk]
-            acc = sums[unfold, blk, s]
-            h = work.tile([P, tokens], F32, name="gate", tag="gate", bufs=14)
-            nc.scalar.activation(out=h[:], in_=acc[:], func=ACT.Sigmoid, bias=const["bias"][:, s : s + 1])
-            gate[unfold, blk, s] = h
+            if s % 2 == 0:
+                gate[unfold, blk, s // 2] = work.tile([P, 2, K_PASS], F32, name="gate", tag="gate", bufs=7)
+            nc.scalar.activation(
+                out=gate[unfold, blk, s // 2][:, s % 2, :], in_=sums[unfold, blk, s][:], func=ACT.Sigmoid, bias=const["bias"][:, s : s + 1]
+            )
 
-        def step_state(unfold, blk, s):
+        def step_state(unfold, blk, r, cols=slice(0, K_PASS)):
             nc.vector.scalar_tensor_tensor(
-                out=rise[blk, s][:], in0=gate[unfold, blk, s][:], scalar=-3.0, in1=gap[blk, s][:], op0=ALU.add, op1=ALU.mult
+                out=rise2[blk, r][:, :, cols], in0=gate[unfold, blk, r][:, :, cols], scalar=-3.0, in1=gap2[blk, r][:, :, cols], op0=ALU.add, op1=ALU.mult
             )
 
         planes = {}
@@ -294,9 +306,9 @@ def tile_liquidtimeconstantfusedtwounfolds_w4_kernel(
             dst = planes[blk, grp][:, t, :]
             factor, shift = const["g_sixth"][:, s : s + 1], const["a_g"][:, s : s + 1]
             if (blk, s) in CAST_ON_VECTOR:
-                nc.vector.tensor_scalar(out=dst, in0=rise[blk, s][:], scalar1=factor, scalar2=shift, op0=ALU.mult, op1=ALU.add)
+                nc.vector.tensor_scalar(out=dst, in0=rise[blk, s], scalar1=factor, scalar2=shift, op0=ALU.mult, op1=ALU.add)
             else:
-                nc.scalar.activation(out=dst, in_=rise[blk, s][:], func=ACT.Identity, scale=factor, bias=shift)
+                nc.scalar.activation(out=dst, in_=rise[blk, s], func=ACT.Identity, scale=factor, bias=shift)
 
         def interleave(blk, grp):
             tile = work.tile([P, P * BLOCK_TILES[blk], PACK], BF16, name="x1_grouped", tag="x1_grouped", align_bytes=64)
@@ -307,31 +319,24 @@ def tile_liquidtimeconstantfusedtwounfolds_w4_kernel(
 
         def next_gap(blk, s):
             if blk in GAP_ON_SCALAR:
-                nc.scalar.activation(out=gap[blk, s][:], in_=rise[blk, s][:], func=ACT.Identity, scale=-1.0 / 36.0, bias=const["a_sixth"][:, s : s + 1])
+                nc.scalar.activation(out=gap[blk, s], in_=rise[blk, s], func=ACT.Identity, scale=-1.0 / 36.0, bias=const["a_sixth"][:, s : s + 1])
                 return
             nc.vector.tensor_scalar(
-                out=gap[blk, s][:], in0=rise[blk, s][:], scalar1=-1.0 / 36.0, scalar2=const["a_sixth"][:, s : s + 1], op0=ALU.mult, op1=ALU.add
+                out=gap[blk, s], in0=rise[blk, s], scalar1=-1.0 / 36.0, scalar2=const["a_sixth"][:, s : s + 1], op0=ALU.mult, op1=ALU.add
             )
 
-        turned_out = {}
-
-        def turn_out(blk, s, j):
-            grp, t = divmod(s, PACK)
-            if t == 0:
-                turned_out[blk, grp, j] = bank([P, PACK, P], "turn")
-            dst = turned_out[blk, grp, j][:, t, :]
-            alone = (blk, grp, j) in EMIT_ON_VECTOR
-            if not alone:
-                nc.tensor.matmul(out=dst, lhsT=const["a"][:, s : s + 1].to_broadcast([P, P]), rhs=identity[:], start=True, stop=False, is_transpose=True)
-            nc.tensor.matmul(out=dst, lhsT=rise[blk, s][:, P * j : P * (j + 1)], rhs=identity[:], start=alone, stop=True, is_transpose=True)
-
-        def store(blk, grp, j):
-            turned = turned_out[blk, grp, j]
-            result = work.tile([P, P, PACK], F32, name="result", tag="result", bufs=6)
-            if (blk, grp, j) in EMIT_ON_VECTOR:
-                a_part = a_rows[:, K_PASS * grp : K_PASS * (grp + 1)].rearrange("p (m t) -> p m t", t=PACK)
-                nc.vector.tensor_tensor(out=result[:], in0=turned[:].rearrange("p t m -> p m t"), in1=a_part, op=ALU.add)
-            elif (blk, grp, j) in COPY_ON_VECTOR:
+        def emit(blk, grp, j):
+            turned = bank([P, PACK, P], "turn")
+            nc.tensor.matmul(
+                out=turned[:].rearrange("p t m -> p (t m)"), lhsT=identity_bf16[:], rhs=const["a_rows"][:, grp, :], start=True, stop=False
+            )
+            for t in range(PACK):
+                nc.tensor.matmul(
+                    out=turned[:, t, :], lhsT=rise[blk, PACK * grp + t][:, P * j : P * (j + 1)], rhs=identity[:],
+                    start=False, stop=(t == PACK - 1), is_transpose=True,
+                )
+            result = work.tile([P, P, PACK], F32, name="result", tag="result", bufs=8)
+            if (blk, grp, j) in COPY_ON_VECTOR:
                 nc.vector.tensor_copy(out=result[:], in_=turned[:].rearrange("p t m -> p m t"))
             else:
                 nc.scalar.copy(out=result[:], in_=turned[:].rearrange("p t m -> p m t"))
@@ -339,54 +344,43 @@ def tile_liquidtimeconstantfusedtwounfolds_w4_kernel(
                 out=rows_of(out, blk)[:, j, K_PASS * grp : K_PASS * (grp + 1)], in_=result[:].rearrange("p m t -> p (m t)")
             )
 
-        def emit(blk, grp, j):
-            for t in range(PACK):
-                turn_out(blk, PACK * grp + t, j)
-            store(blk, grp, j)
-
         def requantise(blk, grp):
             quantise(("x1", blk, grp), regrouped[blk, grp])
 
         parts = [(grp, pair) for pair in range(2) for grp in range(GROUPS)]
 
         constants_scalar()
-        for s in range(PACK):
-            regroup_words(s)
+        regroup_words(0)
         for grp in range(GROUPS):
             turn_x0(0, grp, 0)
-            times_g(0, grp, 0)
             first_gap(0, grp, 0)
         for grp in range(GROUPS):
             turn_x0(0, grp, 1)
         for pair in range(2):
             widen(0, pair)
             turn_inp(0, pair)
+        for grp, pair in parts:
+            times_g(0, grp, pair)
         for grp in range(GROUPS):
-            times_g(0, grp, 1)
             first_gap(0, grp, 1)
         constants_vector()
-        quantise_input(0, 1)
-        regroup_scales(0)
-        quantise_input(0, 2)
         quantise_input(0, 0)
-        regroup_scales(1)
+        regroup_scales(0)
+        quantise_input(0, 1)
+        quantise_input(0, 2)
         for grp in range(GROUPS):
             turn_x0(1, grp, 0)
-            times_g(1, grp, 0)
+        open_early(1, 0)
 
-        def regroup(s):
-            if s >= PACK:
-                regroup_words(s)
-            regroup_scales(s)
-
+        regroup_words(1)
+        regroup_scales(1)
+        first_gap(1, 0, 0)
         beside = {
-            0: [(regroup, 2), (regroup, 3)],
-            1: [(widen, 1, 0), (first_gap, 1, 0, 0), (turn_x0, 1, 0, 1), (regroup, 4)],
-            2: [(turn_inp, 1, 0), (turn_x0, 1, 1, 1), (widen, 1, 1), (regroup, 5)],
-            3: [(first_gap, 1, 1, 0), (turn_inp, 1, 1), (times_g, 1, 0, 1), (times_g, 1, 1, 1), (regroup, 6)],
-            4: [(quantise_input, 1, 1), (regroup, 7)],
-            5: [(first_gap, 1, 0, 1), (quantise_input, 1, 2), (quantise_input, 1, 0)],
-            7: [(first_gap, 1, 1, 1)],
+            0: [(times_g, 1, 0, 0), (times_g, 1, 1, 0), (widen, 1, 0), (widen, 1, 1)],
+            3: [(first_gap, 1, 1, 0), (turn_x0, 1, 0, 1), (turn_x0, 1, 1, 1), (times_g, 1, 0, 1), (times_g, 1, 1, 1)],
+            4: [(turn_inp, 1, 0)],
+            5: [(turn_inp, 1, 1), (quantise_input, 1, 1), (quantise_input, 1, 2), (quantise_input, 1, 0)],
+            7: [(first_gap, 1, 0, 1), (first_gap, 1, 1, 1)],
         }
         for s in range(SLICES):
             multiply(1, 0, s)
@@ -396,35 +390,64 @@ def tile_liquidtimeconstantfusedtwounfolds_w4_kernel(
 
         for s in range(SLICES):
             multiply(1, 1, s)
-        P1 = lambda b, s: (step_state, 1, b, s)
-        P2 = lambda b, s: (step_state, 2, b, s)
-        C = lambda b, s: (cast, b, s)
-        S1 = lambda b, s: (squash, 1, b, s)
-        S2 = lambda b, s: (squash, 2, b, s)
-        M2 = lambda b, s: (multiply, 2, b, s)
-        G = lambda b, s: (next_gap, b, s)
-        I = lambda b, s: (interleave, b, s)
-        Q = lambda b, s: (requantise, b, s)
-        E = lambda b, g, j: (emit, b, g, j)
-        seq = [
-            P1(0,0), P1(0,1), C(0,0), P1(0,2), C(0,1), P1(0,3), C(0,2), S1(1,0), C(0,3), P1(0,4), C(0,4), P1(0,5), C(0,5), I(0,0), S1(1,1), S1(1,2),
-            P1(0,6), C(0,6), Q(0,0), S1(1,3), (open_early, 0), P1(0,7), C(0,7), P1(1,0), C(1,0), P1(1,1), C(1,1), I(0,1), S1(1,4), S1(1,5), P1(1,2), Q(0,1), C(1,2),
-            M2(0,0), M2(0,1), M2(0,2), M2(0,3), M2(0,4), M2(0,5), S1(1,6), M2(0,6),
-            P1(1,3), C(1,3), P1(1,4), C(1,4), P1(1,5), C(1,5), I(1,0), S1(1,7), M2(0,7), S2(0,0), P1(1,6), C(1,6), Q(1,0), S2(0,1), P1(1,7), C(1,7),
-            S2(0,2), S2(0,3), (open_early, 1), G(0,0), G(0,1), G(0,2), I(1,1), P2(0,0), Q(1,1), S2(0,4), S2(0,5), S2(0,6), S2(0,7),
-            M2(1,0), M2(1,1), M2(1,2), M2(1,3), M2(1,4), M2(1,5),
-            G(0,3), P2(0,1), G(0,4), P2(0,2), P2(0,3), S2(1,0), S2(1,1), S2(1,2), S2(1,3), S2(1,4),
-            E(0,0,0), M2(1,6), S2(1,5), E(0,0,1), M2(1,7), S2(1,6), E(0,0,2), S2(1,7), E(0,0,3),
-            G(0,5), P2(0,4), G(0,6), P2(0,5), G(0,7), P2(0,6), G(1,0), P2(0,7),
-            E(0,1,0), E(0,1,1), E(0,1,2), E(0,1,3),
-            G(1,1), P2(1,0), G(1,2), P2(1,1), G(1,3), P2(1,2), G(1,4), P2(1,3),
-            E(1,0,0), E(1,0,1), E(1,0,2), E(1,0,3),
-            G(1,5), P2(1,4), G(1,6), P2(1,5), G(1,7), P2(1,6), P2(1,7),
-        ]
-        for call in seq:
-            call[0](*call[1:])
-        for s in range(PACK, SLICES):
-            for j in range(4):
-                turn_out(1, s, j)
+        for k in range(SLICES):
+            blk, r = divmod(k, PACK)
+            if k != 1:
+                step_state(1, blk, r)
+            if k % 2 == 0 and k > 0:
+                interleave(*divmod(k // 2 - 1, GROUPS))
+            if k % 2 == 1 and k > 1:
+                requantise(*divmod(k // 2 - 1, GROUPS))
+            if k == 0:
+                step_state(1, 0, 1)
+                cast(0, 0)
+                cast(0, 1)
+            if k == SLICES - 1:
+                next_gap(0, 0)
+            if k != 0:
+                cast(blk, 2 * r)
+                cast(blk, 2 * r + 1)
+            if k == 3:
+                open_early(2, 0)
+            if SOFF <= k < SOFF + 4:
+                squash(1, 1, 2 * (k - SOFF))
+                squash(1, 1, 2 * (k - SOFF) + 1)
+            if k == 5:
+                for s in range(SLICES):
+                    multiply(2, 0, s)
+            if k >= 6:
+                squash(2, 0, 2 * (k - 6))
+                squash(2, 0, 2 * (k - 6) + 1)
+        open_early(2, 1)
+        next_gap(0, 1)
+        interleave(1, 1)
+        next_gap(0, 2)
+        requantise(1, 1)
+        next_gap(0, 3)
+        step_state(2, 0, 0)
+        step_state(2, 0, 1)
+        for s in range(4, SLICES):
+            squash(2, 0, s)
+        for s in range(SLICES):
+            multiply(2, 1, s)
+            squash(2, 1, s)
+            if s >= EOFF:
+                emit(0, 0, s - EOFF)
+        next_gap(0, 4)
+        next_gap(0, 5)
+        for k in range(2, SLICES - 2):
+            blk, r = divmod(k, PACK)
+            nb, nr = divmod(k + 1, PACK)
+            next_gap(nb, 2 * nr)
+            next_gap(nb, 2 * nr + 1)
+            step_state(2, blk, r)
+            if k % 2 == 1:
+                for j in range(4):
+                    emit(blk, r // 2, j)
+        next_gap(1, 6)
+        next_gap(1, 7)
+        for half in range(2):
+            for r in range(2, 4):
+                step_state(2, 1, r, slice(PAIR * half, PAIR * (half + 1)))
         for j in range(4):
-            store(1, 1, j)
+            emit(1, 1, j)

@@ -16,438 +16,434 @@ FP8X4 = mybir.dt.float8_e4m3fn_x4
 FP4X4 = mybir.dt.float4_e2m1fn_x4
 ALU = mybir.AluOpType
 ACT = mybir.ActivationFunctionType
+ENGINE = mybir.EngineType
 
 P = 128
 PACK = 4
-K_PASS = P * PACK
-GROUPS = N // K_PASS
+GROUP = P * PACK
+GROUPS = N // GROUP
 SLICES = GROUPS * PACK
-SETS = 1 + GROUPS
-PAIR = 2 * P
+PASSES = 1 + GROUPS
+TILES = 4
+BLOCK = P * TILES
+BLOCKS = B // BLOCK
+HALF = BLOCK // 2
 LN_3_2 = 0.4054651081081644
 
-BLOCK_TILES = (4, 4)
-LAG1 = 2
-LAG2 = 1
-CAST_ON_VECTOR = ((0, 0), (0, 1), (0, 3), (0, 7), (1, 3), (1, 7))
-EARLY = {(1, 0): 3, (1, 1): 0, (2, 0): 4, (2, 1): 4}
-SOFF = 1
-EOFF = 4
-WARM = True
-EMIT_ON_VECTOR = ((1, 1, 1), (1, 1, 3))
-ENG = mybir.EngineType
-MANUAL = {ENG.PE, ENG.SP, ENG.DVE, ENG.Activation}
-COPY_ON_VECTOR = ((1, 1, 1), (1, 1, 3))
-GAP_ON_SCALAR = ()
-BANKS = None
-LAGG = 10
+OPENED_EARLY = {(1, 0): 3, (1, 1): 0, (2, 0): 4, (2, 1): 6}
+
+GATE_BUFS = 8
+PLANE_BUFS = 3
+RESULT_BUFS = 8
 
 
 def tile_liquidtimeconstantfusedtwounfolds_w4_kernel(
     tc, x0, inp_bytes, inp_scale, u_words, u_scales, w_words, w_scales, b, arev, g, out
 ):
     nc = tc.nc
-    blocks = len(BLOCK_TILES)
-    first_row = [P * sum(BLOCK_TILES[:i]) for i in range(blocks)]
 
     def rows_of(hbm, blk):
-        tiles = BLOCK_TILES[blk]
-        return hbm[first_row[blk] : first_row[blk] + P * tiles, :].rearrange("(p j) k -> p j k", j=tiles)
+        return hbm[BLOCK * blk : BLOCK * (blk + 1), :].rearrange("(p j) k -> p j k", j=TILES)
+
+    def half_cols(half):
+        return slice(HALF * half, HALF * (half + 1))
 
     with ExitStack() as ctx:
         keep = ctx.enter_context(tc.tile_pool(name="keep", bufs=1))
-        work = ctx.enter_context(tc.tile_pool(name="work", bufs=3))
+        work = ctx.enter_context(tc.tile_pool(name="work", bufs=PLANE_BUFS))
         psum = ctx.enter_context(tc.psum_pool(name="psum", bufs=8))
+        ctx.enter_context(tc.manual_schedule(engines={ENGINE.PE, ENGINE.SP, ENGINE.DVE, ENGINE.Activation}))
 
-        if MANUAL:
-            ctx.enter_context(tc.manual_schedule(engines=MANUAL))
+        def bank(shape):
+            return psum.tile(shape, F32, name="bank", tag="bank")
 
-        def bank(shape, role):
-            if BANKS is None:
-                return psum.tile(shape, F32, name="bank", tag="bank")
-            return psum.tile(shape, F32, name=role, tag=role, bufs=BANKS[role])
-
-        def per_channel(vec, name):
+        def load_per_channel(vec, name):
             tile = keep.tile([P, GROUPS, PACK], BF16, name=name)
             nc.scalar.dma_start(out=tile[:], in_=vec.rearrange("(g p t) -> p g t", p=P, t=PACK))
             return tile[:].rearrange("p g t -> p (g t)")
 
-        scales_raw = keep.tile([P, SETS, N], U8, name="scales_raw")
+        scales_raw = keep.tile([P, PASSES, N], U8, name="scales_raw")
         nc.vector.memset(scales_raw[:].bitcast(I32), 0)
 
-        g_col = per_channel(g, "g_col")
+        g_col = load_per_channel(g, "g_col")
         identity = keep.tile([P, P], F32, name="identity")
         make_identity(nc, identity[:])
-        identity_bf16 = keep.tile([P, P], BF16, name="identity_bf16")
-        make_identity(nc, identity_bf16[:])
         inp_scale_col = keep.tile([P, PACK], F32, name="inp_scale_col")
         nc.scalar.dma_start(out=inp_scale_col[:], in_=inp_scale.rearrange("o (p t) -> p (o t)", t=PACK))
-        a_col = per_channel(arev, "a_col")
-        b_col = per_channel(b, "b_col")
+        a_col = load_per_channel(arev, "a_col")
+        b_col = load_per_channel(b, "b_col")
 
         x0_rows = {}
         inp_codes = {}
         words_raw = {}
 
-        def load_x0(blk, pair):
-            tile = keep.tile([P, 2, N], BF16, name="x0_rows_%d_%d" % (blk, pair))
-            nc.sync.dma_start(out=tile[:], in_=rows_of(x0, blk)[:, 2 * pair : 2 * pair + 2, :])
-            x0_rows[blk, pair] = tile
+        def load_x0(blk, half):
+            x0_rows[blk, half] = keep.tile([P, 2, N], BF16, name="x0_rows_%d_%d" % (blk, half))
+            nc.sync.dma_start(out=x0_rows[blk, half][:], in_=rows_of(x0, blk)[:, 2 * half : 2 * half + 2, :])
 
-        def load_inp(blk):
-            tile = keep.tile([P, BLOCK_TILES[blk], M], U8, name="inp_codes_%d" % blk)
-            nc.sync.dma_start(out=tile[:], in_=rows_of(inp_bytes, blk))
-            inp_codes[blk] = tile
+        def load_block(blk):
+            load_x0(blk, 0)
+            inp_codes[blk] = keep.tile([P, TILES, M], U8, name="inp_codes_%d" % blk)
+            nc.sync.dma_start(out=inp_codes[blk][:], in_=rows_of(inp_bytes, blk))
+            load_x0(blk, 1)
 
         def load_words(grp):
-            tile = keep.tile([P, SETS, 2 * K_PASS], U8, name="words_raw_%d" % grp)
-            cols = slice(2 * K_PASS * grp, 2 * K_PASS * (grp + 1))
+            tile = keep.tile([P, PASSES, 2 * GROUP], U8, name="words_raw_%d" % grp)
+            cols = slice(2 * GROUP * grp, 2 * GROUP * (grp + 1))
             nc.sync.dma_start(out=tile[:, 0:1, :].bitcast(I32), in_=w_words.rearrange("g p n -> p g n")[:, :, cols].bitcast(I32))
-            nc.sync.dma_start(out=tile[:, 1:SETS, :].bitcast(I32), in_=u_words.rearrange("g p n -> p g n")[:, :, cols].bitcast(I32))
+            nc.sync.dma_start(out=tile[:, 1:PASSES, :].bitcast(I32), in_=u_words.rearrange("g p n -> p g n")[:, :, cols].bitcast(I32))
             words_raw[grp] = tile
 
         def load_scales():
             for quad in range(4):
-                rows = slice(32 * quad, 32 * quad + 4)
+                dst = slice(32 * quad, 32 * quad + 4)
                 src = slice(4 * quad, 4 * quad + 4)
-                nc.sync.dma_start(out=scales_raw[rows, 0:1, :].bitcast(I32), in_=w_scales.rearrange("g q n -> q g n")[src].bitcast(I32))
-                nc.sync.dma_start(out=scales_raw[rows, 1:SETS, :].bitcast(I32), in_=u_scales.rearrange("g q n -> q g n")[src].bitcast(I32))
-
-        def load_block(blk):
-            load_x0(blk, 0)
-            load_inp(blk)
-            for pair in range(1, BLOCK_TILES[blk] // 2):
-                load_x0(blk, pair)
+                nc.sync.dma_start(out=scales_raw[dst, 0:1, :].bitcast(I32), in_=w_scales.rearrange("g q n -> q g n")[src].bitcast(I32))
+                nc.sync.dma_start(out=scales_raw[dst, 1:PASSES, :].bitcast(I32), in_=u_scales.rearrange("g q n -> q g n")[src].bitcast(I32))
 
         load_words(0)
         load_block(0)
         load_scales()
         load_block(1)
         load_words(1)
-        for blk in range(2, blocks):
-            load_block(blk)
 
-
-        if WARM:
-            warm = keep.tile([P, 1], F32, name="warm")
-            nc.scalar.activation(out=warm[:], in_=identity[:, 0:1], func=ACT.Sigmoid)
-
-        def scaled(col, factor, name):
-            tile = keep.tile([P, SLICES], F32, name=name)
-            nc.scalar.activation(out=tile[:], in_=col, func=ACT.Copy, scale=factor)
-            return tile
+        warm_up = keep.tile([P, 1], F32, name="warm_up")
+        nc.scalar.activation(out=warm_up[:], in_=identity[:, 0:1], func=ACT.Sigmoid)
 
         const = {}
 
-        def constants_scalar():
-            spread = bank([P, PACK, P], "turn")
+        def scaled(col, factor, name):
+            const[name] = keep.tile([P, SLICES], F32, name=name)
+            nc.scalar.activation(out=const[name][:], in_=col, func=ACT.Copy, scale=factor)
+
+        def constants_on_scalar():
+            spread = bank([P, PACK, P])
             for t in range(PACK):
                 nc.tensor.transpose(spread[:, t, :], inp_scale_col[:, t : t + 1].to_broadcast([P, P]), identity[:])
-            const["inp_scale"] = keep.tile([P, M], F32, name="inp_scale_rows")
-            nc.scalar.copy(out=const["inp_scale"][:].rearrange("p (m t) -> p m t", t=PACK), in_=spread[:].rearrange("p t m -> p m t"))
-            const["two_a"] = scaled(a_col, 2.0, "two_a")
-            spread_a = psum.tile([P, SLICES, P], BF16, name="bank", tag="bank")
-            for s in range(SLICES):
-                nc.tensor.transpose(spread_a[:, s, :], a_col[:, s : s + 1].to_broadcast([P, P]), identity_bf16[:])
-            const["a_rows"] = keep.tile([P, GROUPS, K_PASS], BF16, name="a_rows")
-            nc.scalar.copy(out=const["a_rows"][:].rearrange("p g n -> p (g n)"), in_=spread_a[:].rearrange("p s m -> p (s m)"))
-            const["a_sixth"] = scaled(a_col, 1.0 / 6.0, "a_sixth")
-            const["g_sixth"] = scaled(g_col, 1.0 / 6.0, "g_sixth")
+            const["inp_scale_rows"] = keep.tile([P, M], F32, name="inp_scale_rows")
+            nc.scalar.copy(
+                out=const["inp_scale_rows"][:].rearrange("p (m t) -> p m t", t=PACK), in_=spread[:].rearrange("p t m -> p m t")
+            )
+            scaled(a_col, 2.0, "two_a")
+            scaled(a_col, 1.0, "a")
+            scaled(a_col, 1.0 / 6.0, "a_sixth")
+            scaled(g_col, 1.0 / 6.0, "g_sixth")
 
-        def constants_vector():
+        def constants_on_vector():
             const["a_g"] = keep.tile([P, SLICES], F32, name="a_g")
             nc.vector.tensor_tensor(out=const["a_g"][:], in0=a_col, in1=g_col, op=ALU.mult)
             const["bias"] = keep.tile([P, SLICES], F32, name="bias")
             nc.vector.tensor_scalar(out=const["bias"][:], in0=b_col, scalar1=LN_3_2, scalar2=None, op0=ALU.add)
 
-        words = [keep.tile([P, PACK, SETS, 2 * P], U8, name="words_%d" % grp, align_bytes=64) for grp in range(GROUPS)]
-        scales = [keep.tile([P, PACK, SETS, P], U8, name="scales_%d" % grp, align_bytes=64) for grp in range(GROUPS)]
+        def of_slice(name, s):
+            return const[name][:, s : s + 1]
+
+        words = [keep.tile([P, PACK, PASSES, 2 * P], U8, name="words_%d" % grp, align_bytes=64) for grp in range(GROUPS)]
+        scales = [keep.tile([P, PACK, PASSES, P], U8, name="scales_%d" % grp, align_bytes=64) for grp in range(GROUPS)]
 
         def regroup_words(grp):
-            src = words_raw[grp][:].rearrange("p s (m t b) -> p t s m b", t=PACK, b=2)
-            nc.vector.tensor_copy(out=words[grp][:].rearrange("p t s (m b) -> p t s m b", b=2), in_=src)
+            src = words_raw[grp][:].rearrange("p i (m t y) -> p t i m y", t=PACK, y=2)
+            nc.vector.tensor_copy(out=words[grp][:].rearrange("p t i (m y) -> p t i m y", y=2), in_=src)
 
         def regroup_scales(grp):
-            src = scales_raw[:].rearrange("p s (g m t) -> p g t s m", g=GROUPS, t=PACK)[:, grp]
+            src = scales_raw[:].rearrange("p i (g m t) -> p g t i m", g=GROUPS, t=PACK)[:, grp]
             nc.vector.tensor_copy(out=scales[grp][:], in_=src)
 
         quantised = {}
 
-        def quantise(key, grouped):
-            tokens = grouped.shape[1]
-            codes = keep.tile([P, tokens], U32, name="codes_%s_%d_%d" % key, align_bytes=64)
-            plane = keep.tile([P, tokens], U8, name="plane_%s_%d_%d" % key, align_bytes=64)
-            nc.vector.quantize_mx(out=codes[:].bitcast(FP8X4), scales=plane[:], in_=grouped[:].rearrange("p c t -> p (c t)"))
-            quantised[key] = (codes, plane)
+        def quantise(key, operand):
+            codes = keep.tile([P, BLOCK], U32, name="codes_%s_%d_%d" % key, align_bytes=64)
+            scale_bytes = keep.tile([P, BLOCK], U8, name="scale_bytes_%s_%d_%d" % key, align_bytes=64)
+            nc.vector.quantize_mx(out=codes[:].bitcast(FP8X4), scales=scale_bytes[:], in_=operand[:].rearrange("p c t -> p (c t)"))
+            quantised[key] = (codes, scale_bytes)
 
         def turn(rows, grp):
-            turned = bank([P, 2, PAIR], "turn")
+            turned = bank([P, 2, HALF])
             for j in range(2):
                 row_words = rows[:, j, :].bitcast(F32)
                 for u in range(2):
                     nc.tensor.transpose(
                         turned[:, u, P * j : P * (j + 1)],
-                        row_words[:, 256 * grp + u : 256 * (grp + 1) : 2],
+                        row_words[:, GROUP // 2 * grp + u : GROUP // 2 * (grp + 1) : 2],
                         identity[:],
                     )
             return turned[:]
 
-        def times_factor(dst, pair, turned, factor):
+        gap = {}
+        rise = {}
+        first_operand = {}
+        for blk in range(BLOCKS):
+            for d in range(SLICES // 2):
+                gap[blk, d] = keep.tile([P, 2, BLOCK], F32, name="gap_%d_%d" % (blk, d))
+                rise[blk, d] = keep.tile([P, 2, BLOCK], F32, name="rise_%d_%d" % (blk, d))
+            for i in range(PASSES):
+                first_operand[blk, i] = keep.tile([P, BLOCK, PACK], BF16, name="first_operand_%d_%d" % (blk, i), align_bytes=64)
+
+        def slice_of(state, blk, s):
+            return state[blk, s // 2][:, s % 2, :]
+
+        inp_rows = {}
+        turned_x0 = {}
+
+        def widen_inp(blk, half):
+            inp_rows[blk, half] = keep.tile([P, 2, M], BF16, name="inp_rows_%d_%d" % (blk, half))
+            for j in range(2):
+                nc.vector.tensor_tensor(
+                    out=inp_rows[blk, half][:, j, :],
+                    in0=inp_codes[blk][:, 2 * half + j, :].bitcast(FP8),
+                    in1=const["inp_scale_rows"][:],
+                    op=ALU.mult,
+                )
+
+        def turn_inp(blk, half):
+            dst = first_operand[blk, 0][:, half_cols(half), :].rearrange("p c t -> p (c t)").bitcast(F32)
+            nc.scalar.copy(out=dst.rearrange("p (c u) -> p c u", u=2), in_=turn(inp_rows[blk, half], 0).rearrange("p u c -> p c u"))
+
+        def turn_x0(blk, grp, half):
+            turned_x0[blk, grp, half] = turn(x0_rows[blk, half], grp).bitcast(BF16).rearrange("p u (c e) -> p c u e", e=2)
+
+        def times_g(blk, grp, half):
+            g_of_group = g_col[:, PACK * grp : PACK * (grp + 1)].rearrange("p (u e) -> p u e", e=2)
             nc.vector.tensor_tensor(
-                out=dst[:, PAIR * pair : PAIR * (pair + 1), :].rearrange("p c (u e) -> p c u e", e=2),
-                in0=turned,
-                in1=factor.rearrange("p (u e) -> p u e", e=2).unsqueeze(1).to_broadcast([P, PAIR, 2, 2]),
+                out=first_operand[blk, 1 + grp][:, half_cols(half), :].rearrange("p c (u e) -> p c u e", e=2),
+                in0=turned_x0[blk, grp, half],
+                in1=g_of_group.unsqueeze(1).to_broadcast([P, HALF, 2, 2]),
                 op=ALU.mult,
             )
 
-        gap = {}
-        rise = {}
-
-        grouped = {}
-        gap2 = {}
-        rise2 = {}
-        wide = {}
-        turned_x0 = {}
-        for blk in range(blocks):
-            tokens = P * BLOCK_TILES[blk]
-            for r in range(SLICES // 2):
-                gap2[blk, r] = keep.tile([P, 2, tokens], F32, name="gap_%d_%d" % (blk, r))
-                rise2[blk, r] = keep.tile([P, 2, tokens], F32, name="rise_%d_%d" % (blk, r))
-                for i in range(2):
-                    gap[blk, 2 * r + i] = gap2[blk, r][:, i, :]
-                    rise[blk, 2 * r + i] = rise2[blk, r][:, i, :]
-            for i in range(SETS):
-                grouped[blk, i] = keep.tile([P, tokens, PACK], BF16, name="grouped_%d_%d" % (blk, i), align_bytes=64)
-
-        def widen(blk, pair):
-            wide[blk, pair] = keep.tile([P, 2, M], BF16, name="wide_%d_%d" % (blk, pair))
-            for j in range(2):
-                nc.vector.tensor_tensor(
-                    out=wide[blk, pair][:, j, :], in0=inp_codes[blk][:, 2 * pair + j, :].bitcast(FP8), in1=const["inp_scale"][:], op=ALU.mult
-                )
-
-        def turn_inp(blk, pair):
-            dst = grouped[blk, 0][:, PAIR * pair : PAIR * (pair + 1), :].rearrange("p c t -> p (c t)").bitcast(F32)
-            nc.scalar.copy(out=dst.rearrange("p (c u) -> p c u", u=2), in_=turn(wide[blk, pair], 0).rearrange("p u c -> p c u"))
-
-        def turn_x0(blk, grp, pair):
-            turned_x0[blk, grp, pair] = turn(x0_rows[blk, pair], grp).bitcast(BF16).rearrange("p u (c e) -> p c u e", e=2)
-
-        def times_g(blk, grp, pair):
-            times_factor(grouped[blk, 1 + grp], pair, turned_x0[blk, grp, pair], g_col[:, PACK * grp : PACK * (grp + 1)])
-
-        def first_gap(blk, grp, pair):
+        def first_gap(blk, grp, half):
             for t in range(PACK):
                 s = PACK * grp + t
                 nc.scalar.activation(
-                    out=gap[blk, s][:, PAIR * pair : PAIR * (pair + 1)],
-                    in_=turned_x0[blk, grp, pair][:, :, t // 2, t % 2],
+                    out=slice_of(gap, blk, s)[:, half_cols(half)],
+                    in_=turned_x0[blk, grp, half][:, :, t // 2, t % 2],
                     func=ACT.Identity,
                     scale=-1.0,
-                    bias=const["two_a"][:, s : s + 1],
+                    bias=of_slice("two_a", s),
                 )
 
-        def quantise_input(blk, i):
-            quantise(("inp", blk, 0) if i == 0 else ("x0", blk, i - 1), grouped[blk, i])
+        def quantise_inp(blk):
+            quantise(("inp", blk, 0), first_operand[blk, 0])
 
-        gate = {}
+        def quantise_x0(blk, grp):
+            quantise(("x0", blk, grp), first_operand[blk, 1 + grp])
+
         sums = {}
+        gate = {}
 
         def passes(unfold, blk, s, first, last):
+            state = "x0" if unfold == 1 else "x1"
+            order = [(0, ("inp", blk, 0))] + [(1 + grp, (state, blk, grp)) for grp in range(GROUPS)]
             if (unfold, blk) == (1, 1):
-                order = [(1, ("x0", blk, 0)), (2, ("x0", blk, 1)), (0, ("inp", blk, 0))]
-            elif unfold == 1:
-                order = [(0, ("inp", blk, 0)), (1, ("x0", blk, 0)), (2, ("x0", blk, 1))]
-            else:
-                order = [(0, ("inp", blk, 0)), (1, ("x1", blk, 0)), (2, ("x1", blk, 1))]
+                order = order[1:] + order[:1]
             if first == 0:
-                sums[unfold, blk, s] = bank([P, K_PASS], "sum")
-            for i in range(first, last):
-                weight, key = order[i]
-                codes, plane = quantised[key]
+                sums[unfold, blk, s] = bank([P, BLOCK])
+            grp, t = divmod(s, PACK)
+            for n in range(first, last):
+                i, key = order[n]
+                codes, scale_bytes = quantised[key]
                 nc.tensor.matmul_mx(
                     out=sums[unfold, blk, s][:],
-                    lhsT=words[s // PACK][:, s % PACK, weight, :].bitcast(FP4X4),
-                    lhsT_scale=scales[s // PACK][:, s % PACK, weight, :],
+                    lhsT=words[grp][:, t, i, :].bitcast(FP4X4),
+                    lhsT_scale=scales[grp][:, t, i, :],
                     rhs=codes[:].bitcast(FP8X4),
-                    rhs_scale=plane[:],
-                    start=(i == 0),
-                    stop=(i == SETS - 1),
+                    rhs_scale=scale_bytes[:],
+                    start=(n == 0),
+                    stop=(n == PASSES - 1),
                 )
 
-        def multiply(unfold, blk, s):
-            early = s < EARLY[unfold, blk]
-            passes(unfold, blk, s, SETS - 1 if early else 0, SETS)
+        def open_early(unfold, blk, first, last):
+            for n in range(PASSES - 1):
+                for s in range(first, last):
+                    passes(unfold, blk, s, n, n + 1)
 
-        def open_early(unfold, blk):
-            for i in range(SETS - 1):
-                for s in range(EARLY[unfold, blk]):
-                    passes(unfold, blk, s, i, i + 1)
+        def multiply(unfold, blk, first, last):
+            for s in range(first, last):
+                passes(unfold, blk, s, PASSES - 1 if s < OPENED_EARLY[unfold, blk] else 0, PASSES)
 
-        def squash(unfold, blk, s):
-            if s % 2 == 0:
-                gate[unfold, blk, s // 2] = work.tile([P, 2, K_PASS], F32, name="gate", tag="gate", bufs=7)
-            nc.scalar.activation(
-                out=gate[unfold, blk, s // 2][:, s % 2, :], in_=sums[unfold, blk, s][:], func=ACT.Sigmoid, bias=const["bias"][:, s : s + 1]
-            )
+        def squash(unfold, blk, first, last):
+            for s in range(first, last):
+                if s % 2 == 0:
+                    gate[unfold, blk, s // 2] = work.tile([P, 2, BLOCK], F32, name="gate", tag="gate", bufs=GATE_BUFS)
+                nc.scalar.activation(
+                    out=gate[unfold, blk, s // 2][:, s % 2, :], in_=sums[unfold, blk, s][:], func=ACT.Sigmoid, bias=of_slice("bias", s)
+                )
 
-        def step_state(unfold, blk, r, cols=slice(0, K_PASS)):
+        def step(unfold, blk, d, cols=slice(0, BLOCK)):
             nc.vector.scalar_tensor_tensor(
-                out=rise2[blk, r][:, :, cols], in0=gate[unfold, blk, r][:, :, cols], scalar=-3.0, in1=gap2[blk, r][:, :, cols], op0=ALU.add, op1=ALU.mult
+                out=rise[blk, d][:, :, cols],
+                in0=gate[unfold, blk, d][:, :, cols],
+                scalar=-3.0,
+                in1=gap[blk, d][:, :, cols],
+                op0=ALU.add,
+                op1=ALU.mult,
             )
 
         planes = {}
-        regrouped = {}
+        second_operand = {}
 
-        def cast(blk, s):
-            grp, t = divmod(s, PACK)
-            if t == 0:
-                planes[blk, grp] = work.tile([P, PACK, P * BLOCK_TILES[blk]], BF16, name="planes", tag="planes")
-            dst = planes[blk, grp][:, t, :]
-            factor, shift = const["g_sixth"][:, s : s + 1], const["a_g"][:, s : s + 1]
-            if (blk, s) in CAST_ON_VECTOR:
-                nc.vector.tensor_scalar(out=dst, in0=rise[blk, s], scalar1=factor, scalar2=shift, op0=ALU.mult, op1=ALU.add)
-            else:
-                nc.scalar.activation(out=dst, in_=rise[blk, s], func=ACT.Identity, scale=factor, bias=shift)
+        def cast(blk, d):
+            for s in (2 * d, 2 * d + 1):
+                grp, t = divmod(s, PACK)
+                if t == 0:
+                    planes[blk, grp] = work.tile([P, PACK, BLOCK], BF16, name="planes", tag="planes")
+                dst, src = planes[blk, grp][:, t, :], slice_of(rise, blk, s)
+                if t == PACK - 1 or (blk, d) == (0, 0):
+                    nc.vector.tensor_scalar(
+                        out=dst, in0=src, scalar1=of_slice("g_sixth", s), scalar2=of_slice("a_g", s), op0=ALU.mult, op1=ALU.add
+                    )
+                else:
+                    nc.scalar.activation(out=dst, in_=src, func=ACT.Identity, scale=of_slice("g_sixth", s), bias=of_slice("a_g", s))
 
         def interleave(blk, grp):
-            tile = work.tile([P, P * BLOCK_TILES[blk], PACK], BF16, name="x1_grouped", tag="x1_grouped", align_bytes=64)
+            tile = work.tile([P, BLOCK, PACK], BF16, name="second_operand", tag="second_operand", align_bytes=64)
             nc.vector.tensor_copy(
                 out=tile[:].rearrange("p (c i) t -> p c t i", i=4), in_=planes[blk, grp][:].rearrange("p t (c i) -> p c t i", i=4)
             )
-            regrouped[blk, grp] = tile
+            second_operand[blk, grp] = tile
 
-        def next_gap(blk, s):
-            if blk in GAP_ON_SCALAR:
-                nc.scalar.activation(out=gap[blk, s], in_=rise[blk, s], func=ACT.Identity, scale=-1.0 / 36.0, bias=const["a_sixth"][:, s : s + 1])
-                return
+        def quantise_x1(blk, grp):
+            quantise(("x1", blk, grp), second_operand[blk, grp])
+
+        def second_gap(blk, s):
             nc.vector.tensor_scalar(
-                out=gap[blk, s], in0=rise[blk, s], scalar1=-1.0 / 36.0, scalar2=const["a_sixth"][:, s : s + 1], op0=ALU.mult, op1=ALU.add
+                out=slice_of(gap, blk, s),
+                in0=slice_of(rise, blk, s),
+                scalar1=-1.0 / 36.0,
+                scalar2=of_slice("a_sixth", s),
+                op0=ALU.mult,
+                op1=ALU.add,
             )
 
-        def emit(blk, grp, j):
-            turned = bank([P, PACK, P], "turn")
-            nc.tensor.matmul(
-                out=turned[:].rearrange("p t m -> p (t m)"), lhsT=identity_bf16[:], rhs=const["a_rows"][:, grp, :], start=True, stop=False
-            )
-            for t in range(PACK):
-                nc.tensor.matmul(
-                    out=turned[:, t, :], lhsT=rise[blk, PACK * grp + t][:, P * j : P * (j + 1)], rhs=identity[:],
-                    start=False, stop=(t == PACK - 1), is_transpose=True,
+        def emit(blk, grp):
+            for j in range(TILES):
+                turned = bank([P, PACK, P])
+                for t in range(PACK):
+                    s = PACK * grp + t
+                    nc.tensor.matmul(
+                        out=turned[:, t, :], lhsT=of_slice("a", s).to_broadcast([P, P]), rhs=identity[:],
+                        start=True, stop=False, is_transpose=True,
+                    )
+                    nc.tensor.matmul(
+                        out=turned[:, t, :], lhsT=slice_of(rise, blk, s)[:, P * j : P * (j + 1)], rhs=identity[:],
+                        start=False, stop=True, is_transpose=True,
+                    )
+                result = work.tile([P, P, PACK], F32, name="result", tag="result", bufs=RESULT_BUFS)
+                if (blk, grp) == (BLOCKS - 1, GROUPS - 1) and j % 2 == 1:
+                    nc.vector.tensor_copy(out=result[:], in_=turned[:].rearrange("p t m -> p m t"))
+                else:
+                    nc.scalar.copy(out=result[:], in_=turned[:].rearrange("p t m -> p m t"))
+                nc.sync.dma_start(
+                    out=rows_of(out, blk)[:, j, GROUP * grp : GROUP * (grp + 1)], in_=result[:].rearrange("p m t -> p (m t)")
                 )
-            result = work.tile([P, P, PACK], F32, name="result", tag="result", bufs=8)
-            if (blk, grp, j) in COPY_ON_VECTOR:
-                nc.vector.tensor_copy(out=result[:], in_=turned[:].rearrange("p t m -> p m t"))
-            else:
-                nc.scalar.copy(out=result[:], in_=turned[:].rearrange("p t m -> p m t"))
-            nc.sync.dma_start(
-                out=rows_of(out, blk)[:, j, K_PASS * grp : K_PASS * (grp + 1)], in_=result[:].rearrange("p m t -> p (m t)")
-            )
 
-        def requantise(blk, grp):
-            quantise(("x1", blk, grp), regrouped[blk, grp])
 
-        parts = [(grp, pair) for pair in range(2) for grp in range(GROUPS)]
-
-        constants_scalar()
+        constants_on_scalar()
         regroup_words(0)
         for grp in range(GROUPS):
             turn_x0(0, grp, 0)
             first_gap(0, grp, 0)
         for grp in range(GROUPS):
             turn_x0(0, grp, 1)
-        for pair in range(2):
-            widen(0, pair)
-            turn_inp(0, pair)
-        for grp, pair in parts:
-            times_g(0, grp, pair)
+        for half in range(2):
+            widen_inp(0, half)
+            turn_inp(0, half)
+        for half in range(2):
+            for grp in range(GROUPS):
+                times_g(0, grp, half)
         for grp in range(GROUPS):
             first_gap(0, grp, 1)
-        constants_vector()
-        quantise_input(0, 0)
+        constants_on_vector()
+        quantise_inp(0)
         regroup_scales(0)
-        quantise_input(0, 1)
-        quantise_input(0, 2)
+        for grp in range(GROUPS):
+            quantise_x0(0, grp)
         for grp in range(GROUPS):
             turn_x0(1, grp, 0)
-        open_early(1, 0)
+        open_early(1, 0, 0, OPENED_EARLY[1, 0])
 
         regroup_words(1)
         regroup_scales(1)
         first_gap(1, 0, 0)
-        beside = {
-            0: [(times_g, 1, 0, 0), (times_g, 1, 1, 0), (widen, 1, 0), (widen, 1, 1)],
-            3: [(first_gap, 1, 1, 0), (turn_x0, 1, 0, 1), (turn_x0, 1, 1, 1), (times_g, 1, 0, 1), (times_g, 1, 1, 1)],
-            4: [(turn_inp, 1, 0)],
-            5: [(turn_inp, 1, 1), (quantise_input, 1, 1), (quantise_input, 1, 2), (quantise_input, 1, 0)],
-            7: [(first_gap, 1, 0, 1), (first_gap, 1, 1, 1)],
-        }
-        for s in range(SLICES):
-            multiply(1, 0, s)
-            squash(1, 0, s)
-            for call in beside.get(s, []):
-                call[0](*call[1:])
-
-        for s in range(SLICES):
-            multiply(1, 1, s)
-        for k in range(SLICES):
-            blk, r = divmod(k, PACK)
-            if k != 1:
-                step_state(1, blk, r)
-            if k % 2 == 0 and k > 0:
-                interleave(*divmod(k // 2 - 1, GROUPS))
-            if k % 2 == 1 and k > 1:
-                requantise(*divmod(k // 2 - 1, GROUPS))
-            if k == 0:
-                step_state(1, 0, 1)
-                cast(0, 0)
-                cast(0, 1)
-            if k == SLICES - 1:
-                next_gap(0, 0)
-            if k != 0:
-                cast(blk, 2 * r)
-                cast(blk, 2 * r + 1)
-            if k == 3:
-                open_early(2, 0)
-            if SOFF <= k < SOFF + 4:
-                squash(1, 1, 2 * (k - SOFF))
-                squash(1, 1, 2 * (k - SOFF) + 1)
-            if k == 5:
-                for s in range(SLICES):
-                    multiply(2, 0, s)
-            if k >= 6:
-                squash(2, 0, 2 * (k - 6))
-                squash(2, 0, 2 * (k - 6) + 1)
-        open_early(2, 1)
-        next_gap(0, 1)
-        interleave(1, 1)
-        next_gap(0, 2)
-        requantise(1, 1)
-        next_gap(0, 3)
-        step_state(2, 0, 0)
-        step_state(2, 0, 1)
-        for s in range(4, SLICES):
-            squash(2, 0, s)
-        for s in range(SLICES):
-            multiply(2, 1, s)
-            squash(2, 1, s)
-            if s >= EOFF:
-                emit(0, 0, s - EOFF)
-        next_gap(0, 4)
-        next_gap(0, 5)
-        for k in range(2, SLICES - 2):
-            blk, r = divmod(k, PACK)
-            nb, nr = divmod(k + 1, PACK)
-            next_gap(nb, 2 * nr)
-            next_gap(nb, 2 * nr + 1)
-            step_state(2, blk, r)
-            if k % 2 == 1:
-                for j in range(4):
-                    emit(blk, r // 2, j)
-        next_gap(1, 6)
-        next_gap(1, 7)
+        for grp in range(GROUPS):
+            times_g(1, grp, 0)
         for half in range(2):
-            for r in range(2, 4):
-                step_state(2, 1, r, slice(PAIR * half, PAIR * (half + 1)))
-        for j in range(4):
-            emit(1, 1, j)
+            widen_inp(1, half)
+        multiply(1, 0, 0, PACK)
+        squash(1, 0, 0, PACK)
+        first_gap(1, 1, 0)
+        for grp in range(GROUPS):
+            turn_x0(1, grp, 1)
+        for grp in range(GROUPS):
+            times_g(1, grp, 1)
+        for half in range(2):
+            multiply(1, 0, PACK + half, PACK + half + 1)
+            squash(1, 0, PACK + half, PACK + half + 1)
+            turn_inp(1, half)
+        for grp in range(GROUPS):
+            quantise_x0(1, grp)
+        quantise_inp(1)
+        multiply(1, 0, SLICES - 2, SLICES)
+        squash(1, 0, SLICES - 2, SLICES)
+        for grp in range(GROUPS):
+            first_gap(1, grp, 1)
+
+        multiply(1, 1, 0, SLICES)
+        step(1, 0, 0)
+        step(1, 0, 1)
+        cast(0, 0)
+        cast(0, 1)
+        step(1, 0, 2)
+        interleave(0, 0)
+        squash(1, 1, 0, 2)
+        cast(0, 2)
+        step(1, 0, 3)
+        quantise_x1(0, 0)
+        squash(1, 1, 2, PACK)
+        cast(0, 3)
+        open_early(2, 0, 0, OPENED_EARLY[2, 0])
+        squash(1, 1, PACK, SLICES)
+        step(1, 1, 0)
+        interleave(0, 1)
+        second_gap(0, 0)
+        quantise_x1(0, 1)
+
+        multiply(2, 0, 0, SLICES)
+        cast(1, 0)
+        step(1, 1, 1)
+        second_gap(0, 1)
+        cast(1, 1)
+        step(1, 1, 2)
+        interleave(1, 0)
+        squash(2, 0, 0, PACK)
+        cast(1, 2)
+        step(1, 1, 3)
+        quantise_x1(1, 0)
+        open_early(2, 1, 0, PACK)
+        cast(1, 3)
+        squash(2, 0, PACK, SLICES)
+        open_early(2, 1, PACK, OPENED_EARLY[2, 1])
+        second_gap(0, 2)
+        interleave(1, 1)
+        second_gap(0, 3)
+        quantise_x1(1, 1)
+
+        multiply(2, 1, 0, OPENED_EARLY[2, 1])
+        step(2, 0, 0)
+        step(2, 0, 1)
+        squash(2, 1, 0, PACK)
+        emit(0, 0)
+        multiply(2, 1, OPENED_EARLY[2, 1], SLICES)
+        squash(2, 1, PACK, SLICES)
+        for blk, grp in ((0, 1), (1, 0)):
+            for t in range(PACK):
+                second_gap(blk, PACK * grp + t)
+            step(2, blk, 2 * grp)
+            step(2, blk, 2 * grp + 1)
+            emit(blk, grp)
+        for s in range(PACK, SLICES):
+            second_gap(1, s)
+        for half in range(2):
+            step(2, 1, 2, half_cols(half))
+            step(2, 1, 3, half_cols(half))
+        emit(1, 1)

@@ -57,21 +57,20 @@ def tile_liquidtimeconstantfusedtwounfolds_w4_kernel(
         def bank(shape):
             return psum.tile(shape, F32, name="bank", tag="bank")
 
-        def load_per_channel(vec, name):
+        def load_per_channel(queue, vec, name):
             tile = keep.tile([P, GROUPS, PACK], BF16, name=name)
-            nc.scalar.dma_start(out=tile[:], in_=vec.rearrange("(g p t) -> p g t", p=P, t=PACK))
+            queue.dma_start(out=tile[:], in_=vec.rearrange("(g p t) -> p g t", p=P, t=PACK))
             return tile[:].rearrange("p g t -> p (g t)")
 
         scales_raw = keep.tile([P, PASSES, N], U8, name="scales_raw")
         nc.vector.memset(scales_raw[:].bitcast(I32), 0)
 
-        g_col = load_per_channel(g, "g_col")
+        g_col = load_per_channel(nc.scalar, g, "g_col")
         identity = keep.tile([P, P], F32, name="identity")
         make_identity(nc, identity[:])
         inp_scale_col = keep.tile([P, PACK], F32, name="inp_scale_col")
         nc.scalar.dma_start(out=inp_scale_col[:], in_=inp_scale.rearrange("o (p t) -> p (o t)", t=PACK))
-        a_col = load_per_channel(arev, "a_col")
-        b_col = load_per_channel(b, "b_col")
+        a_col = load_per_channel(nc.scalar, arev, "a_col")
 
         x0_rows = {}
         inp_codes = {}
@@ -81,11 +80,9 @@ def tile_liquidtimeconstantfusedtwounfolds_w4_kernel(
             x0_rows[blk, half] = keep.tile([P, 2, N], BF16, name="x0_rows_%d_%d" % (blk, half))
             nc.sync.dma_start(out=x0_rows[blk, half][:], in_=rows_of(x0, blk)[:, 2 * half : 2 * half + 2, :])
 
-        def load_block(blk):
-            load_x0(blk, 0)
+        def load_inp(blk):
             inp_codes[blk] = keep.tile([P, TILES, M], U8, name="inp_codes_%d" % blk)
             nc.sync.dma_start(out=inp_codes[blk][:], in_=rows_of(inp_bytes, blk))
-            load_x0(blk, 1)
 
         def load_words(grp):
             tile = keep.tile([P, PASSES, 2 * GROUP], U8, name="words_raw_%d" % grp)
@@ -102,13 +99,15 @@ def tile_liquidtimeconstantfusedtwounfolds_w4_kernel(
                 nc.sync.dma_start(out=scales_raw[dst, 1:PASSES, :].bitcast(I32), in_=u_scales.rearrange("g q n -> q g n")[src].bitcast(I32))
 
         load_words(0)
-        load_block(0)
+        load_x0(0, 0)
+        load_inp(0)
+        load_x0(0, 1)
         load_scales()
-        load_block(1)
+        b_col = load_per_channel(nc.sync, b, "b_col")
+        load_x0(1, 0)
+        load_inp(1)
+        load_x0(1, 1)
         load_words(1)
-
-        warm_up = keep.tile([P, 1], F32, name="warm_up")
-        nc.scalar.activation(out=warm_up[:], in_=identity[:, 0:1], func=ACT.Sigmoid)
 
         const = {}
 
@@ -117,6 +116,10 @@ def tile_liquidtimeconstantfusedtwounfolds_w4_kernel(
             nc.scalar.activation(out=const[name][:], in_=col, func=ACT.Copy, scale=factor)
 
         def constants_on_scalar():
+            scaled(a_col, 2.0, "two_a")
+            scaled(a_col, 1.0, "a")
+            scaled(a_col, 1.0 / 6.0, "a_sixth")
+            scaled(g_col, 1.0 / 6.0, "g_sixth")
             spread = bank([P, PACK, P])
             for t in range(PACK):
                 nc.tensor.transpose(spread[:, t, :], inp_scale_col[:, t : t + 1].to_broadcast([P, P]), identity[:])
@@ -124,10 +127,6 @@ def tile_liquidtimeconstantfusedtwounfolds_w4_kernel(
             nc.scalar.copy(
                 out=const["inp_scale_rows"][:].rearrange("p (m t) -> p m t", t=PACK), in_=spread[:].rearrange("p t m -> p m t")
             )
-            scaled(a_col, 2.0, "two_a")
-            scaled(a_col, 1.0, "a")
-            scaled(a_col, 1.0 / 6.0, "a_sixth")
-            scaled(g_col, 1.0 / 6.0, "g_sixth")
 
         def constants_on_vector():
             const["a_g"] = keep.tile([P, SLICES], F32, name="a_g")
@@ -348,8 +347,8 @@ def tile_liquidtimeconstantfusedtwounfolds_w4_kernel(
         for half in range(2):
             widen_inp(0, half)
             turn_inp(0, half)
-        for half in range(2):
-            for grp in range(GROUPS):
+        for grp in range(GROUPS):
+            for half in range(2):
                 times_g(0, grp, half)
         for grp in range(GROUPS):
             first_gap(0, grp, 1)
@@ -362,24 +361,24 @@ def tile_liquidtimeconstantfusedtwounfolds_w4_kernel(
             turn_x0(1, grp, 0)
         open_early(1, 0, 0, OPENED_EARLY[1, 0])
 
+        for half in range(2):
+            widen_inp(1, half)
         regroup_words(1)
         regroup_scales(1)
         first_gap(1, 0, 0)
         for grp in range(GROUPS):
             times_g(1, grp, 0)
-        for half in range(2):
-            widen_inp(1, half)
         multiply(1, 0, 0, PACK)
         squash(1, 0, 0, PACK)
-        first_gap(1, 1, 0)
+        for half in range(2):
+            turn_inp(1, half)
         for grp in range(GROUPS):
             turn_x0(1, grp, 1)
+        first_gap(1, 1, 0)
         for grp in range(GROUPS):
             times_g(1, grp, 1)
-        for half in range(2):
-            multiply(1, 0, PACK + half, PACK + half + 1)
-            squash(1, 0, PACK + half, PACK + half + 1)
-            turn_inp(1, half)
+        multiply(1, 0, PACK, PACK + 2)
+        squash(1, 0, PACK, PACK + 2)
         for grp in range(GROUPS):
             quantise_x0(1, grp)
         quantise_inp(1)

from contextlib import ExitStack

import concourse.mybir as mybir
from concourse.masks import make_identity

B, N, M = 1024, 1024, 512
FLOPS = 2 * B * N * (M + 2 * N)

F32 = mybir.dt.float32
BF16 = mybir.dt.bfloat16
I32 = mybir.dt.int32
U32 = mybir.dt.uint32
U8 = mybir.dt.uint8
FP8 = mybir.dt.float8_e4m3fn
FP8X4 = mybir.dt.float8_e4m3fn_x4
FP4X4 = mybir.dt.float4_e2m1fn_x4
ALU = mybir.AluOpType
ACT = mybir.ActivationFunctionType
ENGINE = mybir.EngineType

P = 128
PACK = 4
GROUP = P * PACK
GROUPS = N // GROUP
SLICES = GROUPS * PACK
PASSES = 1 + GROUPS
TILES = 4
BLOCK = P * TILES
BLOCKS = B // BLOCK
HALF = BLOCK // 2
LN_3_2 = 0.4054651081081644

OPENED_EARLY = {(1, 0): 3, (1, 1): 0, (2, 0): 4, (2, 1): 6}

GATE_BUFS = 8
PLANE_BUFS = 3
RESULT_BUFS = 8


def tile_liquidtimeconstantfusedtwounfolds_w4_kernel(
    tc, x0, inp_bytes, inp_scale, u_words, u_scales, w_words, w_scales, b, arev, g, out
):
    nc = tc.nc

    def rows_of(hbm, blk):
        return hbm[BLOCK * blk : BLOCK * (blk + 1), :].rearrange("(p j) k -> p j k", j=TILES)

    def half_cols(half):
        return slice(HALF * half, HALF * (half + 1))

    with ExitStack() as ctx:
        keep = ctx.enter_context(tc.tile_pool(name="keep", bufs=1))
        work = ctx.enter_context(tc.tile_pool(name="work", bufs=PLANE_BUFS))
        psum = ctx.enter_context(tc.psum_pool(name="psum", bufs=8))
        ctx.enter_context(tc.manual_schedule(engines={ENGINE.PE, ENGINE.SP, ENGINE.DVE, ENGINE.Activation}))

        def bank(shape):
            return psum.tile(shape, F32, name="bank", tag="bank")

        def load_per_channel(queue, vec, name):
            tile = keep.tile([P, GROUPS, PACK], BF16, name=name)
            queue.dma_start(out=tile[:], in_=vec.rearrange("(g p t) -> p g t", p=P, t=PACK))
            return tile[:].rearrange("p g t -> p (g t)")

        scales_raw = keep.tile([P, PASSES, N], U8, name="scales_raw")
        nc.vector.memset(scales_raw[:].bitcast(I32), 0)

        g_col = load_per_channel(nc.scalar, g, "g_col")
        identity = keep.tile([P, P], F32, name="identity")
        make_identity(nc, identity[:])
        inp_scale_col = keep.tile([P, PACK], F32, name="inp_scale_col")
        nc.scalar.dma_start(out=inp_scale_col[:], in_=inp_scale.rearrange("o (p t) -> p (o t)", t=PACK))
        a_col = load_per_channel(nc.scalar, arev, "a_col")

        x0_rows = {}
        inp_codes = {}
        words_raw = {}

        def load_x0(blk, half):
            x0_rows[blk, half] = keep.tile([P, 2, N], BF16, name="x0_rows_%d_%d" % (blk, half))
            nc.sync.dma_start(out=x0_rows[blk, half][:], in_=rows_of(x0, blk)[:, 2 * half : 2 * half + 2, :])

        def load_inp(blk):
            inp_codes[blk] = keep.tile([P, TILES, M], U8, name="inp_codes_%d" % blk)
            nc.sync.dma_start(out=inp_codes[blk][:], in_=rows_of(inp_bytes, blk))

        def load_words(grp):
            tile = keep.tile([P, PASSES, 2 * GROUP], U8, name="words_raw_%d" % grp)
            cols = slice(2 * GROUP * grp, 2 * GROUP * (grp + 1))
            nc.sync.dma_start(out=tile[:, 0:1, :].bitcast(I32), in_=w_words.rearrange("g p n -> p g n")[:, :, cols].bitcast(I32))
            nc.sync.dma_start(out=tile[:, 1:PASSES, :].bitcast(I32), in_=u_words.rearrange("g p n -> p g n")[:, :, cols].bitcast(I32))
            words_raw[grp] = tile

        def load_scales():
            for quad in range(4):
                dst = slice(32 * quad, 32 * quad + 4)
                src = slice(4 * quad, 4 * quad + 4)
                nc.sync.dma_start(out=scales_raw[dst, 0:1, :].bitcast(I32), in_=w_scales.rearrange("g q n -> q g n")[src].bitcast(I32))
                nc.sync.dma_start(out=scales_raw[dst, 1:PASSES, :].bitcast(I32), in_=u_scales.rearrange("g q n -> q g n")[src].bitcast(I32))

        load_words(0)
        load_x0(0, 0)
        load_inp(0)
        load_x0(0, 1)
        load_scales()
        b_col = load_per_channel(nc.sync, b, "b_col")
        load_x0(1, 0)
        load_inp(1)
        load_x0(1, 1)
        load_words(1)

        const = {}

        def scaled(col, factor, name):
            const[name] = keep.tile([P, SLICES], F32, name=name)
            nc.scalar.activation(out=const[name][:], in_=col, func=ACT.Copy, scale=factor)

        def constants_on_scalar():
            scaled(a_col, 2.0, "two_a")
            scaled(a_col, 1.0, "a")
            scaled(a_col, 1.0 / 6.0, "a_sixth")
            scaled(g_col, 1.0 / 6.0, "g_sixth")
            spread = bank([P, PACK, P])
            for t in range(PACK):
                nc.tensor.transpose(spread[:, t, :], inp_scale_col[:, t : t + 1].to_broadcast([P, P]), identity[:])
            const["inp_scale_rows"] = keep.tile([P, M], F32, name="inp_scale_rows")
            nc.scalar.copy(
                out=const["inp_scale_rows"][:].rearrange("p (m t) -> p m t", t=PACK), in_=spread[:].rearrange("p t m -> p m t")
            )

        def constants_on_vector():
            const["a_g"] = keep.tile([P, SLICES], F32, name="a_g")
            nc.vector.tensor_tensor(out=const["a_g"][:], in0=a_col, in1=g_col, op=ALU.mult)
            const["bias"] = keep.tile([P, SLICES], F32, name="bias")
            nc.vector.tensor_scalar(out=const["bias"][:], in0=b_col, scalar1=LN_3_2, scalar2=None, op0=ALU.add)

        def of_slice(name, s):
            return const[name][:, s : s + 1]

        words = [keep.tile([P, PACK, PASSES, 2 * P], U8, name="words_%d" % grp, align_bytes=64) for grp in range(GROUPS)]
        scales = [keep.tile([P, PACK, PASSES, P], U8, name="scales_%d" % grp, align_bytes=64) for grp in range(GROUPS)]

        def regroup_words(grp):
            src = words_raw[grp][:].rearrange("p i (m t y) -> p t i m y", t=PACK, y=2)
            nc.vector.tensor_copy(out=words[grp][:].rearrange("p t i (m y) -> p t i m y", y=2), in_=src)

        def regroup_scales(grp):
            src = scales_raw[:].rearrange("p i (g m t) -> p g t i m", g=GROUPS, t=PACK)[:, grp]
            nc.vector.tensor_copy(out=scales[grp][:], in_=src)

        quantised = {}

        def quantise(key, operand):
            codes = keep.tile([P, BLOCK], U32, name="codes_%s_%d_%d" % key, align_bytes=64)
            scale_bytes = keep.tile([P, BLOCK], U8, name="scale_bytes_%s_%d_%d" % key, align_bytes=64)
            nc.vector.quantize_mx(out=codes[:].bitcast(FP8X4), scales=scale_bytes[:], in_=operand[:].rearrange("p c t -> p (c t)"))
            quantised[key] = (codes, scale_bytes)

        def turn(rows, grp):
            turned = bank([P, 2, HALF])
            for j in range(2):
                row_words = rows[:, j, :].bitcast(F32)
                for u in range(2):
                    nc.tensor.transpose(
                        turned[:, u, P * j : P * (j + 1)],
                        row_words[:, GROUP // 2 * grp + u : GROUP // 2 * (grp + 1) : 2],
                        identity[:],
                    )
            return turned[:]

        gap = {}
        rise = {}
        first_operand = {}
        for blk in range(BLOCKS):
            for d in range(SLICES // 2):
                gap[blk, d] = keep.tile([P, 2, BLOCK], F32, name="gap_%d_%d" % (blk, d))
                rise[blk, d] = keep.tile([P, 2, BLOCK], F32, name="rise_%d_%d" % (blk, d))
            for i in range(PASSES):
                first_operand[blk, i] = keep.tile([P, BLOCK, PACK], BF16, name="first_operand_%d_%d" % (blk, i), align_bytes=64)

        def slice_of(state, blk, s):
            return state[blk, s // 2][:, s % 2, :]

        inp_rows = {}
        turned_x0 = {}

        def widen_inp(blk, half):
            inp_rows[blk, half] = keep.tile([P, 2, M], BF16, name="inp_rows_%d_%d" % (blk, half))
            for j in range(2):
                nc.vector.tensor_tensor(
                    out=inp_rows[blk, half][:, j, :],
                    in0=inp_codes[blk][:, 2 * half + j, :].bitcast(FP8),
                    in1=const["inp_scale_rows"][:],
                    op=ALU.mult,
                )

        def turn_inp(blk, half):
            dst = first_operand[blk, 0][:, half_cols(half), :].rearrange("p c t -> p (c t)").bitcast(F32)
            nc.scalar.copy(out=dst.rearrange("p (c u) -> p c u", u=2), in_=turn(inp_rows[blk, half], 0).rearrange("p u c -> p c u"))

        def turn_x0(blk, grp, half):
            turned_x0[blk, grp, half] = turn(x0_rows[blk, half], grp).bitcast(BF16).rearrange("p u (c e) -> p c u e", e=2)

        def times_g(blk, grp, half):
            g_of_group = g_col[:, PACK * grp : PACK * (grp + 1)].rearrange("p (u e) -> p u e", e=2)
            nc.vector.tensor_tensor(
                out=first_operand[blk, 1 + grp][:, half_cols(half), :].rearrange("p c (u e) -> p c u e", e=2),
                in0=turned_x0[blk, grp, half],
                in1=g_of_group.unsqueeze(1).to_broadcast([P, HALF, 2, 2]),
                op=ALU.mult,
            )

        def first_gap(blk, grp, half):
            for t in range(PACK):
                s = PACK * grp + t
                nc.scalar.activation(
                    out=slice_of(gap, blk, s)[:, half_cols(half)],
                    in_=turned_x0[blk, grp, half][:, :, t // 2, t % 2],
                    func=ACT.Identity,
                    scale=-1.0,
                    bias=of_slice("two_a", s),
                )

        def quantise_inp(blk):
            quantise(("inp", blk, 0), first_operand[blk, 0])

        def quantise_x0(blk, grp):
            quantise(("x0", blk, grp), first_operand[blk, 1 + grp])

        sums = {}
        gate = {}

        def passes(unfold, blk, s, first, last):
            state = "x0" if unfold == 1 else "x1"
            order = [(0, ("inp", blk, 0))] + [(1 + grp, (state, blk, grp)) for grp in range(GROUPS)]
            if (unfold, blk) == (1, 1):
                order = order[1:] + order[:1]
            if first == 0:
                sums[unfold, blk, s] = bank([P, BLOCK])
            grp, t = divmod(s, PACK)
            for n in range(first, last):
                i, key = order[n]
                codes, scale_bytes = quantised[key]
                nc.tensor.matmul_mx(
                    out=sums[unfold, blk, s][:],
                    lhsT=words[grp][:, t, i, :].bitcast(FP4X4),
                    lhsT_scale=scales[grp][:, t, i, :],
                    rhs=codes[:].bitcast(FP8X4),
                    rhs_scale=scale_bytes[:],
                    start=(n == 0),
                    stop=(n == PASSES - 1),
                )

        def open_early(unfold, blk, first, last):
            for n in range(PASSES - 1):
                for s in range(first, last):
                    passes(unfold, blk, s, n, n + 1)

        def multiply(unfold, blk, first, last):
            for s in range(first, last):
                passes(unfold, blk, s, PASSES - 1 if s < OPENED_EARLY[unfold, blk] else 0, PASSES)

        def squash(unfold, blk, first, last):
            for s in range(first, last):
                if s % 2 == 0:
                    gate[unfold, blk, s // 2] = work.tile([P, 2, BLOCK], F32, name="gate", tag="gate", bufs=GATE_BUFS)
                nc.scalar.activation(
                    out=gate[unfold, blk, s // 2][:, s % 2, :], in_=sums[unfold, blk, s][:], func=ACT.Sigmoid, bias=of_slice("bias", s)
                )

        def step(unfold, blk, d, cols=slice(0, BLOCK)):
            nc.vector.scalar_tensor_tensor(
                out=rise[blk, d][:, :, cols],
                in0=gate[unfold, blk, d][:, :, cols],
                scalar=-3.0,
                in1=gap[blk, d][:, :, cols],
                op0=ALU.add,
                op1=ALU.mult,
            )

        planes = {}
        second_operand = {}

        def cast(blk, d):
            for s in (2 * d, 2 * d + 1):
                grp, t = divmod(s, PACK)
                if t == 0:
                    planes[blk, grp] = work.tile([P, PACK, BLOCK], BF16, name="planes", tag="planes")
                dst, src = planes[blk, grp][:, t, :], slice_of(rise, blk, s)
                if t == PACK - 1 or (blk, d) == (0, 0):
                    nc.vector.tensor_scalar(
                        out=dst, in0=src, scalar1=of_slice("g_sixth", s), scalar2=of_slice("a_g", s), op0=ALU.mult, op1=ALU.add
                    )
                else:
                    nc.scalar.activation(out=dst, in_=src, func=ACT.Identity, scale=of_slice("g_sixth", s), bias=of_slice("a_g", s))

        def interleave(blk, grp):
            tile = work.tile([P, BLOCK, PACK], BF16, name="second_operand", tag="second_operand", align_bytes=64)
            nc.vector.tensor_copy(
                out=tile[:].rearrange("p (c i) t -> p c t i", i=4), in_=planes[blk, grp][:].rearrange("p t (c i) -> p c t i", i=4)
            )
            second_operand[blk, grp] = tile

        def quantise_x1(blk, grp):
            quantise(("x1", blk, grp), second_operand[blk, grp])

        def second_gap(blk, s):
            nc.vector.tensor_scalar(
                out=slice_of(gap, blk, s),
                in0=slice_of(rise, blk, s),
                scalar1=-1.0 / 36.0,
                scalar2=of_slice("a_sixth", s),
                op0=ALU.mult,
                op1=ALU.add,
            )

        def emit(blk, grp):
            for j in range(TILES):
                turned = bank([P, PACK, P])
                for t in range(PACK):
                    s = PACK * grp + t
                    nc.tensor.matmul(
                        out=turned[:, t, :], lhsT=of_slice("a", s).to_broadcast([P, P]), rhs=identity[:],
                        start=True, stop=False, is_transpose=True,
                    )
                    nc.tensor.matmul(
                        out=turned[:, t, :], lhsT=slice_of(rise, blk, s)[:, P * j : P * (j + 1)], rhs=identity[:],
                        start=False, stop=True, is_transpose=True,
                    )
                result = work.tile([P, P, PACK], F32, name="result", tag="result", bufs=RESULT_BUFS)
                if (blk, grp) == (BLOCKS - 1, GROUPS - 1) and j % 2 == 1:
                    nc.vector.tensor_copy(out=result[:], in_=turned[:].rearrange("p t m -> p m t"))
                else:
                    nc.scalar.copy(out=result[:], in_=turned[:].rearrange("p t m -> p m t"))
                nc.sync.dma_start(
                    out=rows_of(out, blk)[:, j, GROUP * grp : GROUP * (grp + 1)], in_=result[:].rearrange("p m t -> p (m t)")
                )


        constants_on_scalar()
        regroup_words(0)
        for grp in range(GROUPS):
            turn_x0(0, grp, 0)
            first_gap(0, grp, 0)
        for grp in range(GROUPS):
            turn_x0(0, grp, 1)
        for half in range(2):
            widen_inp(0, half)
            turn_inp(0, half)
        for grp in range(GROUPS):
            for half in range(2):
                times_g(0, grp, half)
        for grp in range(GROUPS):
            first_gap(0, grp, 1)
        constants_on_vector()
        quantise_inp(0)
        regroup_scales(0)
        for grp in range(GROUPS):
            quantise_x0(0, grp)
        for grp in range(GROUPS):
            turn_x0(1, grp, 0)
        open_early(1, 0, 0, OPENED_EARLY[1, 0])

        for half in range(2):
            widen_inp(1, half)
        regroup_words(1)
        regroup_scales(1)
        first_gap(1, 0, 0)
        for grp in range(GROUPS):
            times_g(1, grp, 0)
        multiply(1, 0, 0, PACK)
        squash(1, 0, 0, PACK)
        for half in range(2):
            turn_inp(1, half)
        for grp in range(GROUPS):
            turn_x0(1, grp, 1)
        first_gap(1, 1, 0)
        for grp in range(GROUPS):
            times_g(1, grp, 1)
        multiply(1, 0, PACK, PACK + 2)
        squash(1, 0, PACK, PACK + 2)
        for grp in range(GROUPS):
            quantise_x0(1, grp)
        quantise_inp(1)
        multiply(1, 0, SLICES - 2, SLICES)
        squash(1, 0, SLICES - 2, SLICES)
        for grp in range(GROUPS):
            first_gap(1, grp, 1)

        multiply(1, 1, 0, SLICES)
        step(1, 0, 0)
        step(1, 0, 1)
        cast(0, 0)
        cast(0, 1)
        step(1, 0, 2)
        interleave(0, 0)
        squash(1, 1, 0, 2)
        cast(0, 2)
        step(1, 0, 3)
        quantise_x1(0, 0)
        squash(1, 1, 2, PACK)
        cast(0, 3)
        open_early(2, 0, 0, OPENED_EARLY[2, 0])
        squash(1, 1, PACK, SLICES)
        step(1, 1, 0)
        interleave(0, 1)
        second_gap(0, 0)
        quantise_x1(0, 1)

        multiply(2, 0, 0, SLICES)
        cast(1, 0)
        step(1, 1, 1)
        second_gap(0, 1)
        cast(1, 1)
        step(1, 1, 2)
        interleave(1, 0)
        squash(2, 0, 0, PACK)
        cast(1, 2)
        step(1, 1, 3)
        quantise_x1(1, 0)
        open_early(2, 1, 0, PACK)
        cast(1, 3)
        squash(2, 0, PACK, SLICES)
        open_early(2, 1, PACK, OPENED_EARLY[2, 1])
        second_gap(0, 2)
        interleave(1, 1)
        second_gap(0, 3)
        quantise_x1(1, 1)

        multiply(2, 1, 0, OPENED_EARLY[2, 1])
        step(2, 0, 0)
        step(2, 0, 1)
        squash(2, 1, 0, PACK)
        emit(0, 0)
        multiply(2, 1, OPENED_EARLY[2, 1], SLICES)
        squash(2, 1, PACK, SLICES)
        for blk, grp in ((0, 1), (1, 0)):
            for t in range(PACK):
                second_gap(blk, PACK * grp + t)
            step(2, blk, 2 * grp)
            step(2, blk, 2 * grp + 1)
            emit(blk, grp)
        for s in range(PACK, SLICES):
            second_gap(1, s)
        for half in range(2):
            step(2, 1, 2, half_cols(half))
            step(2, 1, 3, half_cols(half))
        emit(1, 1)
